import numpy as np, ml_dtypes
CORES = [3,11,19,27,35,43,51,59]
N = 8
BF = ml_dtypes.bfloat16
B, S, D, SH = 2, 8192, 4096, 5
W, BC = N * B, 16
LAST = (2 * 255 * 255) >> SH
def middle(m):
    return 16 * (m % 16) + 8, 16 * (m // 16) + 8
def index(p, x, y):
    return ((x - int(p[0])) ** 2 + (y - int(p[1])) ** 2) >> SH
def loud(d, rng, cells):
    t = rng.integers(0, S, (N, 8)); sg = rng.choice(np.array([-15.0, 15.0]), 16); v = d["tr"].reshape(N, 8, 16, S); x, y = middle(np.array(cells))
    ld = sg - np.sign(sg) * rng.integers(0, 2, (N, 8, 16))
    for q in range(N):
        for g in range(8):
            d["tau"][q, g, index(d["pos"][q, g], x, y)] = t[q, g]; v[q, g, :, t[q, g]] = ld[q, g].astype(BF)
    return t, ld
def setup_inputs(rng):
    tr = rng.integers(-15, 16, (N, 128, S), dtype=np.int8).astype(np.float32).astype(BF)
    pos = rng.integers(0, 256, (N, 8, 2)).astype(np.int32)
    t = np.floor(np.sqrt(np.arange(D) / D) * (rng.random((N, 8, 1)) * 0.5 + 0.25) * S).astype(np.int64) + rng.integers(0, S // 4, (N, 8, D))
    return {"tr": tr, "pos": pos, "tau": t.astype(np.int32)}
def setup_inputs_ends(rng):
    d = setup_inputs(rng); c = np.array([[0, 0], [0, 255], [255, 0], [255, 255]])
    d["pos"] = np.stack([c[rng.permutation(8) % 4] for q in range(N)]).astype(np.int32)
    t = rng.integers(0, S, (N, 8, D)); t[:, :, 0] = 0; t[:, :, LAST] = S - 1; d["tau"] = t.astype(np.int32)
    e = rng.integers(0, 2, W); e[0] = 0; e[W - 1] = 1
    loud(d, rng, np.arange(W) * BC + e * (BC - 1)); return d
def setup_inputs_ties(rng):
    d = setup_inputs(rng); s = int(rng.integers(0, 3)); cells = []
    for k in range(W):
        z = (k + s) % 3; o = [0, BC - 1] if z == 0 else rng.choice(BC, 2, replace=False) if z == 1 else range(BC)
        cells += [k * BC + int(i) for i in o]
    loud(d, rng, cells); return d
def setup_inputs_close(rng):
    d = setup_inputs(rng); k = np.arange(W); lo = k * BC + rng.integers(0, BC // 2, W); hi = k * BC + BC // 2 + rng.integers(0, BC // 2, W); x, y = middle(lo)
    d["pos"][k % N, k // N, 0] = x; d["pos"][k % N, k // N, 1] = y
    t, ld = loud(d, rng, np.concatenate([lo, hi])); v = d["tr"].reshape(N, 8, 16, S); m = np.abs(np.sum(ld, axis=(0, 1)))
    for i in range(W):
        q, g = i % N, i // N; u = (int(t[q, g]) + int(rng.integers(1, S))) % S; h = ld[q, g].copy(); s = int(rng.integers(0, 16))
        if i % 2:
            z = [(m[a] - m[b], a, b) for a in range(16) for b in range(16) if m[a] > m[b] + 1 and abs(h[b]) < 15]
            if z:
                s, b = min(z)[1:]; h[b] = h[b] + np.sign(h[b])
        h[s] = h[s] - np.sign(h[s])
        d["tau"][q, g, 0] = u; v[q, g, :, u] = h.astype(BF)
    return d
def setup_inputs_steps(rng):
    d = setup_inputs(rng); d["pos"] = np.repeat(rng.integers(0, 256, (N, 1, 2)), 8, axis=1).astype(np.int32)
    d["tau"] = np.repeat(rng.integers(0, S, (N, 8, D // 64)), 64, axis=2).astype(np.int32); return d
def setup_inputs_spread(rng):
    d = setup_inputs(rng); a = rng.choice(np.array([0, 1, 4, 15], np.int8), (N, 8, 1, S))
    v = np.clip(rng.integers(-15, 16, (N, 8, 16, S), dtype=np.int8), -a, a)
    d["tr"] = v.reshape(N, 128, S).astype(np.float32).astype(BF)
    d["pos"] = np.floor(256 * rng.random((N, 8, 2)) ** 3).astype(np.int32); d["tau"] = np.floor(S * rng.random((N, 8, D)) ** 3).astype(np.int32); return d
def check_inputs(d):
    bad = []; v = np.asarray(d["tr"]).astype(np.float32)
    if not ((np.abs(v) <= 15) & (np.rint(v) == v)).all(): bad.append("samples")
    if not ((d["pos"] >= 0) & (d["pos"] <= 255)).all(): bad.append("places")
    if not ((d["tau"] >= 0) & (d["tau"] < S)).all(): bad.append("times")
    return bad
def focus(v, pos, tau, x, y):
    a = np.zeros((16, len(x)), np.int64)
    for q in range(N):
        for g in range(8): a += v[q, g][:, tau[q, g][index(pos[q, g], x, y)]]
    return a
def reference(tr, pos, tau):
    v = tr.astype(np.float32).astype(np.int32).reshape(N, 8, 16, S)
    x, y = middle(np.arange(256)); c = focus(v, pos, tau, x, y)
    e = np.sum(c * c, axis=0).reshape(W, BC)
    w = np.arange(W) * BC + np.argmax(e, axis=1)
    j = np.arange(256); x = (16 * (w % 16)[:, None] + j % 16).reshape(-1); y = (16 * (w // 16)[:, None] + j // 16).reshape(-1)
    fine = focus(v, pos, tau, x, y).reshape(16, N, B * 256).transpose(1, 0, 2)
    return {"y": np.ascontiguousarray(fine).astype(np.float32), "w": np.tile(w.reshape(1, 1, W), (N, 1, 1)).astype(np.float32)}

@@ -1,0 +1,360 @@
+from concourse.bass import DstId, RemoteDMATransfer
+from concourse.mybir import AluOpType as A, ActivationFunctionType as F
+
+SCRATCH = {
+    "posi": ("sbuf", [128, 2], "int32"),
+    "posf": ("sbuf", [128, 2], "bfloat16"),
+    "negp": ("sbuf", [128, 2], "float32"),
+    "nps": ("sbuf", [128, 2], "float32"),
+    "taus": ("sbuf", [128, 256], "int32"),
+    "tauo": ("sbuf", [128, 256], "uint16"),
+    "trs": ("sbuf", [128, 8192], "bfloat16"),
+    "comp": ("sbuf", [128, 4096], "bfloat16"),
+    "nat": ("sbuf", [128, 4096], "bfloat16"),
+    "jt": ("sbuf", [128, 4096], "float32"),
+    "e8a": ("sbuf", [128, 128], "bfloat16"),
+    "e8b": ("sbuf", [128, 128], "bfloat16"),
+    "e8": ("sbuf", [128, 128], "bfloat16"),
+    "ones": ("sbuf", [128, 128], "bfloat16"),
+    "onesf": ("sbuf", [128, 128], "float32"),
+    "ident": ("sbuf", [128, 128], "bfloat16"),
+    "g16a": ("sbuf", [128, 128], "float32"),
+    "g16": ("sbuf", [128, 128], "float32"),
+    "wd": ("sbuf", [128, 240], "bfloat16"),
+    "wdi": ("sbuf", [128, 16], "int32"),
+    "wdm": ("sbuf", [128, 16], "int32"),
+    "wf": ("sbuf", [128, 136], "bfloat16"),
+    "wfi": ("sbuf", [128, 136], "int32"),
+    "wfm": ("sbuf", [128, 136], "int32"),
+    "pcol": ("sbuf", [128, 2], "int32"),
+    "rcol": ("sbuf", [128, 2], "int32"),
+    "c16": ("sbuf", [128, 2], "float32"),
+    "rm8": ("sbuf", [128, 2], "float32"),
+    "hcol": ("sbuf", [128, 2], "float32"),
+    "bx": ("sbuf", [128, 2], "float32"),
+    "dyw": ("sbuf", [128, 2], "float32"),
+    "yy": ("sbuf", [128, 256], "float32"),
+    "xx": ("sbuf", [128, 256], "float32"),
+    "yrow": ("sbuf", [128, 256], "float32"),
+    "sx0": ("sbuf", [128, 256], "float32"),
+    "sx": ("sbuf", [128, 256], "float32"),
+    "sy": ("sbuf", [128, 256], "float32"),
+    "sw": ("sbuf", [128, 16], "float32"),
+    "d2w": ("sbuf", [128, 16], "int32"),
+    "lo32": ("sbuf", [128, 16], "int32"),
+    "lo": ("sbuf", [128, 16], "uint16"),
+    "hd": ("sbuf", [128, 256], "int32"),
+    "hm": ("sbuf", [128, 256], "float32"),
+    "prod": ("sbuf", [128, 256], "float32"),
+    "dg": ("sbuf", [128, 256], "float32"),
+    "dd": ("sbuf", [128, 256], "float32"),
+    "a1": ("sbuf", [128, 128], "float32"),
+    "a2": ("sbuf", [128, 64], "float32"),
+    "a3": ("sbuf", [128, 32], "float32"),
+    "a4": ("sbuf", [128, 16], "float32"),
+    "nl": ("sbuf", [128, 16], "uint16"),
+    "dy2": ("sbuf", [128, 256], "float32"),
+    "dx2": ("sbuf", [128, 16], "float32"),
+    "dxs": ("sbuf", [128, 16], "float32"),
+    "vc": ("sbuf", [128, 256], "bfloat16"),
+    "cland": ("sbuf", [128, 256], "bfloat16"),
+    "sq": ("sbuf", [128, 32], "float32"),
+    "one32": ("sbuf", [128, 32], "float32"),
+    "reset": ("sbuf", [128, 32], "float32"),
+    "run": ("sbuf", [128, 32], "float32"),
+    "lt": ("sbuf", [128, 32], "float32"),
+    "acol": ("sbuf", [128, 8], "float32"),
+    "m256": ("sbuf", [128, 8], "float32"),
+    "mask8": ("sbuf", [128, 8], "float32"),
+    "rr": ("sbuf", [128, 16], "bfloat16"),
+    "base": ("sbuf", [128, 16], "bfloat16"),
+    "offu": ("sbuf", [128, 16], "uint16"),
+    "wc": ("sbuf", [128, 16], "float32"),
+    "w1": ("sbuf", [128, 16], "float32"),
+    "w2": ("sbuf", [128, 16], "float32"),
+    "flist": ("sbuf", [128, 256], "uint16"),
+    "ff": ("sbuf", [128, 4096], "bfloat16"),
+    "fsend": ("sbuf", [128, 448], "bfloat16"),
+    "fland": ("sbuf", [128, 512], "bfloat16"),
+    "ysb": ("sbuf", [128, 64], "float32"),
+}
+for _k in range(8):
+    SCRATCH["p%d" % _k] = ("psum", [128, 512], "float32")
+SEMAPHORES = ["carr", "far0", "far1", "far2", "far3", "csent", "fsent"] + ["e%d" % _k for _k in range(140)]
+
+
+def rank_program(g, core, T, topo):
+    rank = T.rank_of(core)
+    if rank is None:
+        return
+    N = len(T.cores)
+    queues = {"G": g, "V": g.vector, "S": g.scalar, "P": g.tensor, "Y": g.sync}
+    known = {q: set() for q in queues}
+    events = []
+
+    def event():
+        e = {"n": len(events), "sem": T.sem["e%d" % len(events)], "total": 0, "knows": set(), "used": False}
+        events.append(e)
+        return e
+
+    def use(q, waits):
+        for e in waits:
+            if e["n"] not in known[q]:
+                queues[q].wait_ge(e["sem"], e["total"])
+                e["used"] = True
+                known[q] |= e["knows"] | {e["n"]}
+
+    def run(q, waits, call, ev=None, inc=1):
+        use(q, waits)
+        e = event() if ev is None else ev
+        assert not e["used"]
+        call().then_inc(e["sem"], inc)
+        e["total"] += inc
+        e["knows"] |= known[q]
+        return e
+
+    def V(waits, fn, *a, **k):
+        return run("V", waits, lambda: fn(*a), **k)
+
+    vec, sca, pe = g.vector, g.scalar, g.tensor
+    ts, tt = vec.tensor_scalar, vec.tensor_tensor
+    act = lambda waits, out, in_, func, **k: run("S", waits, lambda: sca.activation(out, in_, func, **k))
+
+    def chain(waits, mms):
+        use("P", waits)
+        for m in mms:
+            last = m()
+        e = event()
+        last.then_inc(e["sem"], 1)
+        e["total"] = 1
+        e["knows"] |= known["P"]
+        return e
+
+    p = [T["p%d" % k] for k in range(8)]
+
+    e_pos = run("Y", [], lambda: g.sync.dma_start(T.posi[0:8, :], T.pos[:, :]), inc=16)
+    e_tau = run("S", [], lambda: g.scalar.dma_start(T.taus[:, :], T.tau[:, :]), inc=16)
+    e_tr = run("Y", [], lambda: g.sync.dma_start(T.trs[:, :], T.tr[:, :]), inc=16)
+
+    e_e8a = V([], vec.memset, T.e8a[0:8, :], -1.0)
+    e_onesf = V([], vec.memset, T.onesf[:, :], 1.0)
+    e_ones = V([], vec.memset, T.ones[:, :], 1.0)
+    e_one32 = V([], vec.memset, T.one32[:, :], 1.0)
+    e_m256 = V([], vec.memset, T.m256[:, :], 256.0)
+    e_wd0 = V([], vec.memset, T.wd[:, :], 0.0)
+
+    iota_f = lambda out, pat, base: run("G", [], lambda: g.iota(out, pat, base, 0, allow_small_or_imprecise_dtypes=True))
+    sel = lambda waits, out, in_, pat, op, base, cm: run("G", waits, lambda: g.affine_select(out, in_, pat, op, 0.0, base, cm))
+    e_pcol = run("G", [], lambda: g.iota(T.pcol[:, 0:1], [[1, 1]], 0, 1))
+    e_e8b = sel([e_e8a], T.e8b[0:8, :], T.e8a[0:8, :], [[1, 128]], A.is_ge, 0, -16)
+    e_e8 = sel([e_e8b], T.e8[0:8, :], T.e8b[0:8, :], [[-1, 128]], A.is_ge, 15, 16)
+    e_yy = iota_f(T.yy[:, :], [[0, 16], [16, 16]], 8)
+    e_xx = iota_f(T.xx[:, :], [[16, 16], [0, 16]], 8)
+    e_yrow = iota_f(T.yrow[:, :], [[1, 256]], 0)
+    e_g16a = sel([e_onesf], T.g16a[:, :], T.onesf[:, :], [[-16, 8], [0, 16]], A.is_ge, 0, 1)
+    e_g16 = sel([e_g16a], T.g16[:, :], T.g16a[:, :], [[16, 8], [0, 16]], A.is_ge, 15, -1)
+    e_wdi = run("G", [], lambda: g.iota(T.wdi[:, :], [[1, 16]], 128, -1))
+    e_ident = sel([e_ones], T.ident[:, :], T.ones[:, :], [[-1, 128]], A.is_equal, 0, 1)
+    e_wfi = run("G", [], lambda: g.iota(T.wfi[:, :], [[1, 136]], 1024 - 7, -8))
+    e_reset = sel([e_one32], T.reset[:, :], T.one32[:, :], [[0, 2], [1, 16]], A.not_equal, 0, 0)
+    e_mask8 = sel([e_m256], T.mask8[:, :], T.m256[:, :], [[-16, 8]], A.is_equal, 0, 1)
+
+    e_r = V([e_pcol], ts, T.rcol[:, 0:1], T.pcol[:, 0:1], 15, None, A.bitwise_and)
+    e_c16 = V([e_r], ts, T.c16[:, 0:1], T.rcol[:, 0:1], 16.0, 8.0, A.mult, A.add)
+    e_rm8 = V([e_r], ts, T.rm8[:, 0:1], T.rcol[:, 0:1], -8.0, None, A.add)
+    e_hcol = V([e_r], ts, T.hcol[:, 0:1], T.rcol[:, 0:1], -1.0, -4095.5 / 8192, A.mult, A.add)
+
+    e_posf = V([e_pos], vec.tensor_copy, T.posf[0:8, :], T.posi[0:8, :])
+    e_pb = run("P", [e_e8, e_posf], lambda: pe.matmul(p[0][:, 0:2], T.e8[0:8, :], T.posf[0:8, :], start=True, stop=True))
+    root = 8192.0 ** -0.5
+    e_np = V([e_pb], vec.tensor_copy, T.negp[:, :], p[0][:, 0:2])
+    e_nps = V([e_np], ts, T.nps[:, :], T.negp[:, :], root, None, A.mult)
+    nx, ny = T.negp[:, 0:1], T.negp[:, 1:2]
+    e_bx = V([e_rm8], tt, T.bx[:, 0:1], T.rm8[:, 0:1], nx, A.add)
+
+    e_sw = act([e_yy, e_np], T.sw[:, :], T.yy[:, 0:16], F.Square, bias=nx)
+    e_dyw = act([e_c16], T.dyw[:, 0:1], T.c16[:, 0:1], F.Square, bias=ny)
+    e_dx2 = act([e_bx], T.dx2[:, :], T.yy[:, 0:16], F.Square, bias=T.bx[:, 0:1])
+    e_sx0 = act([e_xx, e_nps], T.sx0[:, :], T.xx[:, :], F.Square, bias=T.nps[:, 0:1], scale=root)
+    e_sy = act([], T.sy[:, :], T.yy[:, :], F.Square, bias=T.nps[:, 1:2], scale=root)
+    e_sx = act([e_sx0, e_hcol], T.sx[:, :], T.sx0[:, :], F.Identity, bias=T.hcol[:, 0:1])
+    e_dy2 = act([e_yrow], T.dy2[:, :], T.yrow[:, :], F.Square, bias=ny)
+
+    e_d2w = V([e_sw, e_dyw], ts, T.d2w[:, :], T.sw[:, :], T.dyw[:, 0:1], None, A.add)
+    e_lo32 = V([e_d2w], ts, T.lo32[:, :], T.d2w[:, :], 5, 255, A.arith_shift_right, A.bitwise_and)
+    e_lo = V([e_lo32], vec.tensor_copy, T.lo[:, :], T.lo32[:, :])
+    e_dxs = V([e_dx2], ts, T.dxs[:, :], T.dx2[:, :], -15.5, 1.0 / 32, A.add, A.mult)
+    e_dg = V([e_xx, e_c16], ts, T.dg[:, :], T.xx[:, :], T.c16[:, 0:1], None, A.is_equal)
+    e_hd = V([e_sx, e_sy], tt, T.hd[:, :], T.sx[:, :], T.sy[:, :], A.add)
+    e_hm = V([e_hd], ts, T.hm[:, :], T.hd[:, :], 0.0, None, A.is_equal)
+    e_prod = V([e_hm, e_lo, e_tau], lambda: tt(T.prod[:, :], T.taus[:, :].indirect(T.lo[:, :]), T.hm[:, :], A.mult))
+    e_s = run("P", [e_prod, e_g16], lambda: pe.matmul(p[1][:, 0:256], T.g16[:, :], T.prod[:, :], start=True, stop=True))
+
+    e_jv, e_ja = event(), event()
+    NJ = 3
+
+    def table(q, a):
+        o = T.jt[:, 256 * a:256 * a + 256]
+        if q == "V":
+            V([e_dxs, e_dy2], ts, o, T.dy2[:, :], 1.0 / 32, T.dxs[:, a:a + 1], A.mult, A.add, ev=e_jv)
+        else:
+            run("S", [e_dxs, e_dy2], lambda: sca.activation(o, T.dy2[:, :], F.Identity, bias=T.dxs[:, a:a + 1], scale=1.0 / 32), ev=e_ja)
+
+    for a in range(NJ):
+        table("V", a)
+    for a in range(NJ, 16):
+        table("S", a)
+    e_dd = V([e_s, e_dg], tt, T.dd[:, :], p[1][:, 0:256], T.dg[:, :], A.mult)
+    e_t, src, n = e_dd, T.dd, 256
+    for dst in (T.a1, T.a2, T.a3, T.a4):
+        n //= 2
+        e_t = V([e_t], tt, dst[:, :], src[:, 0:n], src[:, n:2 * n], A.add)
+        src = dst
+    e_nl = V([e_t], vec.tensor_copy, T.nl[:, :], T.a4[:, :])
+    e_wdm = V([e_wdi], ts, T.wdm[:, :], T.wdi[:, :], 15, None, A.bitwise_and)
+    e_wd = V([e_wdm, e_wd0], ts, T.wd[:, 112:128], T.wdm[:, :], 0.0, None, A.is_equal)
+    e_tauo = V([e_tau], vec.tensor_copy, T.tauo[:, :], T.taus[:, :])
+    e_base = V([e_yy, e_rm8], ts, T.base[:, :], T.yy[:, 0:16], T.rm8[:, 0:1], None, A.add)
+    e_wc = V([e_yy], ts, T.wc[0:1, :], T.yy[0:1, 0:16], -8.0, 15.9375 / 16, A.add, A.mult)
+    e_wfm = V([e_wfi], ts, T.wfm[:, :], T.wfi[:, :], 127, None, A.bitwise_and)
+    e_wf = V([e_wfm], ts, T.wf[:, :], T.wfm[:, :], 0.0, None, A.is_equal)
+
+    e_vc = act([e_tr, e_nl], T.vc[:, :], T.trs[:, :].indirect(T.nl[:, :]), F.Copy)
+    e_cs = chain([e_vc, e_wd], [lambda k=k: pe.matmul(p[2][:, 0:32], T.wd[:, 112 - 16 * k:240 - 16 * k], T.vc[:, 32 * k:32 * k + 32],
+                                                      start=k == 0, stop=k == 7) for k in range(8)])
+    own = slice(32 * rank, 32 * rank + 32)
+    e_own = act([e_cs], T.cland[:, own], p[2][:, 0:32], F.Copy)
+
+    others = [(rank + 1 + t) % N for t in range(N - 1)]
+
+    def dst_id(q):
+        rid, pid, _ = topo.addr(T.cores[q])
+        return DstId(rid=rid, pnc=pid)
+
+    def bits(es):
+        m = 0
+        for e in es:
+            m |= 1 << e
+        return m
+
+    eng = [e for e in topo.engines(core, T.cores[others[0]]) if all(e in topo.engines(core, T.cores[q]) for q in others)]
+    use("G", [e_own])
+    g.remote_dma_fused([RemoteDMATransfer(dst_ids=[dst_id(q) for q in others], dma_engine_mask=bits(eng), remote_sem=T.sem.carr,
+                                          srcs=[T.cland[:, own]], dsts=[T.cland[:, own] for q in others])], local_sem=T.sem.csent)
+    n_csent = len(eng)
+
+    h = 136
+    e_cv = V([e_tr, e_tauo], lambda: vec.tensor_copy(T.comp[:, 0:16 * h], T.trs[:, :].indirect(T.tauo[:, 0:h])))
+    e_ca = act([e_tr, e_tauo], T.comp[:, 16 * h:4096], T.trs[:, :].indirect(T.tauo[:, h:256]), F.Copy)
+    e_nv, e_na = event(), event()
+    nv = 10
+    for r in range(nv):
+        V([e_cv, e_ca], vec.tensor_copy, T.nat[:, 256 * r:256 * r + 256], T.comp[:, r::16], ev=e_nv)
+    for r in range(nv, 16):
+        run("S", [e_cv, e_ca], lambda: sca.activation(T.nat[:, 256 * r:256 * r + 256], T.comp[:, r::16], F.Copy), ev=e_na)
+
+    use("P", [e_own, e_ident, e_base, e_ones])
+    pe.matmul(p[5][:, 0:16], T.ident[:, :], T.base[:, :], start=True, stop=False)
+    pe.matmul(p[3][:, 0:32], T.ident[:, :], T.cland[:, own], start=True, stop=False)
+    pe.wait_ge(T.sem.carr, (N - 1) * len(eng))
+    e_tot = chain([], [lambda i=i, q=q: pe.matmul(p[3][:, 0:32], T.ident[:, :], T.cland[:, 32 * q:32 * q + 32], start=False, stop=i == N - 2)
+                       for i, q in enumerate(others)])
+    e_sq = act([e_tot], T.sq[:, :], p[3][:, 0:32], F.Square)
+    e_e = chain([e_sq, e_g16], [lambda: pe.matmul(p[4][:, 0:32], T.g16[:, :], T.sq[:, :], start=True, stop=True)])
+    e_run = V([e_e, e_reset], vec.tensor_tensor_scan, T.run[:, :], T.reset[:, :], p[4][:, 0:32], 0.0, A.mult, A.max)
+    e_r2 = []
+    for b in range(2):
+        e_a = act([e_run], T.lt[:, 16 * b:16 * b + 16], T.run[:, 16 * b:16 * b + 16], F.Sign, bias=T.run[:, 16 * b + 15:16 * b + 16], scale=-1.0,
+                  accum_out=T.acol[:, 4 * b:4 * b + 1])
+        e_r2.append(V([e_a, e_mask8], ts, T.rr[:, b::2], T.mask8[:, :], T.acol[:, 4 * b:4 * b + 1], None, A.mult))
+    e_off = chain(e_r2, [lambda: pe.matmul(p[5][:, 0:16], T.ones[:, :], T.rr[:, :], start=False, stop=True)])
+    e_offu = V([e_off], vec.tensor_copy, T.offu[:, :], p[5][:, 0:16])
+
+    def select(q0, q1):
+        return V([e_offu, e_jv, e_ja], lambda: vec.tensor_copy(T.flist[:, 32 * q0:32 * q1], T.jt[:, :].indirect(T.offu[:, 2 * q0:2 * q1])))
+
+    order = others + [rank]
+    e_sel = {}
+    bank = [0, 1, 2, 3, 4, 6, 7]
+    e_f = {}
+
+    def gather(t):
+        q = order[t]
+        o = 512 * q
+        e1 = V([e_sel[q], e_na, e_nv], lambda: vec.tensor_copy(T.ff[:, o:o + 256], T.nat[:, :].indirect(T.flist[:, 32 * q:32 * q + 16])))
+        e2 = act([e_sel[q], e_nv, e_na], T.ff[:, o + 256:o + 512], T.nat[:, :].indirect(T.flist[:, 32 * q + 16:32 * q + 32]), F.Copy)
+        e_f[t] = (e1, e2)
+
+    e_pt = {}
+
+    def sensors(t):
+        q = order[t]
+        out = p[5] if t == 7 else p[bank[t]]
+        use("P", [e_f[t][0], e_wf])
+        for c in range(8):
+            if c == 4:
+                use("P", [e_f[t][1]])
+            mm = pe.matmul(out[:, 0:64], T.wf[:, 7 - c:135 - c], T.ff[:, 512 * q + 64 * c:512 * q + 64 * c + 64], start=c == 0, stop=t < 7 and c == 7)
+        if t < 7:
+            e_pt[t] = chain([], [lambda: mm])
+
+    e_cp = {}
+
+    def take(t, q):
+        o, i = T.fsend[:, 64 * t:64 * t + 64], p[bank[t]][:, 0:64]
+        if q == "V":
+            e_cp[t] = V([e_pt[t]], vec.tensor_copy, o, i)
+        else:
+            e_cp[t] = act([e_pt[t]], o, i, F.Copy)
+
+    def send(tt_, k):
+        use("G", [e_cp[t] for t in tt_])
+        n = len(eng) // len(tt_)
+        own_f = slice(64 * rank, 64 * rank + 64)
+        g.remote_dma_fused([RemoteDMATransfer(dst_ids=[dst_id(order[t])], dma_engine_mask=bits(eng[n * i:n * i + n]), remote_sem=T.sem["far%d" % k],
+                                              srcs=[T.fsend[:, 64 * t:64 * t + 64]], dsts=[T.fland[:, own_f]]) for i, t in enumerate(tt_)],
+                           local_sem=T.sem.fsent)
+
+    groups = [[0], [1, 2], [3, 4], [5, 6]]
+    for t in (0, 1):
+        e_sel[order[t]] = select(order[t], order[t] + 1)
+    gather(0)
+    sensors(0)
+    gather(1)
+    sensors(1)
+    runs = []
+    for q in order[2:]:
+        if runs and runs[-1][1] == q:
+            runs[-1][1] = q + 1
+        else:
+            runs.append([q, q + 1])
+    for q0, q1 in runs:
+        e = select(q0, q1)
+        for q in range(q0, q1):
+            e_sel[q] = e
+    take(0, "S")
+    send([0], 0)
+    for t in range(2, 8):
+        gather(t)
+        sensors(t)
+        take(t - 1, "V" if t % 2 else "S")
+        if t % 2:
+            send(groups[t // 2], t // 2)
+    e_w1 = V([e_offu], ts, T.w1[0:1, :], T.offu[0:1, :], 1.0 / 256, None, A.mult)
+    e_w2 = V([e_w1, e_wc], tt, T.w2[0:1, :], T.w1[0:1, :], T.wc[0:1, :], A.add)
+    e_w = run("Y", [e_w2], lambda: g.sync.dma_start(T.w[:, :], T.w2[0:1, :]), inc=16)
+
+    for k, tt_ in enumerate(groups):
+        pe.wait_ge(T.sem["far%d" % k], len(eng))
+        for t in tt_:
+            q = (rank - 1 - t) % N
+            mm = pe.matmul(p[5][:, 0:64], T.ident[:, :], T.fland[:, 64 * q:64 * q + 64], start=False, stop=t == 6)
+    e_fin = chain([], [lambda: mm])
+    e_y = V([e_fin], vec.tensor_copy, T.ysb[:, :], p[5][:, 0:64])
+    e_st = run("Y", [e_y], lambda: g.sync.dma_start(T.y[:, :], T.ysb[:, :]), inc=16)
+    use("Y", [e_w, e_st])
+    g.wait_ge(T.sem.csent, n_csent)
+    g.wait_ge(T.sem.fsent, len(groups) * len(eng))
+    for e in events:
+        if not e["used"]:
+            g.wait_ge(e["sem"], e["total"])

@@ -1,86 +1,21 @@
 from concourse.bass import DstId, RemoteDMATransfer
 from concourse.mybir import AluOpType as A, ActivationFunctionType as F
 
-SCRATCH = {
-    "posi": ("sbuf", [128, 2], "int32"),
-    "posf": ("sbuf", [128, 2], "bfloat16"),
-    "negp": ("sbuf", [128, 2], "float32"),
-    "nps": ("sbuf", [128, 2], "float32"),
-    "taus": ("sbuf", [128, 256], "int32"),
-    "tauo": ("sbuf", [128, 256], "uint16"),
-    "trs": ("sbuf", [128, 8192], "bfloat16"),
-    "comp": ("sbuf", [128, 4096], "bfloat16"),
-    "nat": ("sbuf", [128, 4096], "bfloat16"),
-    "jt": ("sbuf", [128, 4096], "float32"),
-    "e8a": ("sbuf", [128, 128], "bfloat16"),
-    "e8b": ("sbuf", [128, 128], "bfloat16"),
-    "e8": ("sbuf", [128, 128], "bfloat16"),
-    "ones": ("sbuf", [128, 128], "bfloat16"),
-    "onesf": ("sbuf", [128, 128], "float32"),
-    "ident": ("sbuf", [128, 128], "bfloat16"),
-    "g16a": ("sbuf", [128, 128], "float32"),
-    "g16": ("sbuf", [128, 128], "float32"),
-    "wd": ("sbuf", [128, 240], "bfloat16"),
-    "wdi": ("sbuf", [128, 16], "int32"),
-    "wdm": ("sbuf", [128, 16], "int32"),
-    "wf": ("sbuf", [128, 136], "bfloat16"),
-    "wfi": ("sbuf", [128, 136], "int32"),
-    "wfm": ("sbuf", [128, 136], "int32"),
-    "pcol": ("sbuf", [128, 2], "int32"),
-    "rcol": ("sbuf", [128, 2], "int32"),
-    "c16": ("sbuf", [128, 2], "float32"),
-    "rm8": ("sbuf", [128, 2], "float32"),
-    "hcol": ("sbuf", [128, 2], "float32"),
-    "bx": ("sbuf", [128, 2], "float32"),
-    "dyw": ("sbuf", [128, 2], "float32"),
-    "yy": ("sbuf", [128, 256], "float32"),
-    "xx": ("sbuf", [128, 256], "float32"),
-    "yrow": ("sbuf", [128, 256], "float32"),
-    "sx0": ("sbuf", [128, 256], "float32"),
-    "sx": ("sbuf", [128, 256], "float32"),
-    "sy": ("sbuf", [128, 256], "float32"),
-    "sw": ("sbuf", [128, 16], "float32"),
-    "d2w": ("sbuf", [128, 16], "int32"),
-    "lo32": ("sbuf", [128, 16], "int32"),
-    "lo": ("sbuf", [128, 16], "uint16"),
-    "hd": ("sbuf", [128, 256], "int32"),
-    "hm": ("sbuf", [128, 256], "float32"),
-    "prod": ("sbuf", [128, 256], "float32"),
-    "dg": ("sbuf", [128, 256], "float32"),
-    "dd": ("sbuf", [128, 256], "float32"),
-    "a1": ("sbuf", [128, 128], "float32"),
-    "a2": ("sbuf", [128, 64], "float32"),
-    "a3": ("sbuf", [128, 32], "float32"),
-    "a4": ("sbuf", [128, 16], "float32"),
-    "nl": ("sbuf", [128, 16], "uint16"),
-    "dy2": ("sbuf", [128, 256], "float32"),
-    "dx2": ("sbuf", [128, 16], "float32"),
-    "dxs": ("sbuf", [128, 16], "float32"),
-    "vc": ("sbuf", [128, 256], "bfloat16"),
-    "cland": ("sbuf", [128, 256], "bfloat16"),
-    "sq": ("sbuf", [128, 32], "float32"),
-    "one32": ("sbuf", [128, 32], "float32"),
-    "reset": ("sbuf", [128, 32], "float32"),
-    "run": ("sbuf", [128, 32], "float32"),
-    "lt": ("sbuf", [128, 32], "float32"),
-    "acol": ("sbuf", [128, 8], "float32"),
-    "m256": ("sbuf", [128, 8], "float32"),
-    "mask8": ("sbuf", [128, 8], "float32"),
-    "rr": ("sbuf", [128, 16], "bfloat16"),
-    "base": ("sbuf", [128, 16], "bfloat16"),
-    "offu": ("sbuf", [128, 16], "uint16"),
-    "wc": ("sbuf", [128, 16], "float32"),
-    "w1": ("sbuf", [128, 16], "float32"),
-    "w2": ("sbuf", [128, 16], "float32"),
-    "flist": ("sbuf", [128, 256], "uint16"),
-    "ff": ("sbuf", [128, 4096], "bfloat16"),
-    "fsend": ("sbuf", [128, 448], "bfloat16"),
-    "fland": ("sbuf", [128, 512], "bfloat16"),
-    "ysb": ("sbuf", [128, 64], "float32"),
+_SB = {
+    "int32": "posi 2 taus 256 vi 128 e8s 128 pgi 2 wdi 16 wdm 16 wfi 68 wfm 68 pcol 2 rcol 2 r4 2 d2w 16 lo32 16 d2i 256 hi 256",
+    "uint16": "tauo 256 lo 16 nl 16 offu 16 flist 256",
+    "bfloat16": "posf 2 trs 8192 comp 4096 nat 4096 e8 128 ones 128 ident 128 wd 144 wf 68 vc 256 cland 256 rr 16 base 32 "
+                "ff 4096 fsend 448 fland 512",
+    "float32": "negp 2 jt 4096 l0 128 l1 128 l2 128 l3 128 pgf 2 pf 2 rf 2 c16 2 c4 2 rm8 2 bx 2 dyw 2 yy 256 xx 256 yrow 256 sy 256 t1 16 sw 16 "
+               "hm 256 prod 256 dg 64 dd 64 a3 32 a4 16 dy2 256 dx2 16 dxs 16 sq 32 one32 32 reset 32 run 32 lt 32 acol 8 "
+               "m256 8 mask16 16 wc 16 w1 16 w2 16 ysb 128",
 }
-for _k in range(8):
-    SCRATCH["p%d" % _k] = ("psum", [128, 512], "float32")
-SEMAPHORES = ["carr", "far0", "far1", "far2", "far3", "csent", "fsent"] + ["e%d" % _k for _k in range(140)]
+SCRATCH = {"p%d" % _k: ("psum", [128, 512], "float32") for _k in range(8)}
+for _d in _SB:
+    _l = _SB[_d].split()
+    for _k in range(0, len(_l), 2):
+        SCRATCH[_l[_k]] = ("sbuf", [128, int(_l[_k + 1])], _d)
+SEMAPHORES = ["carr", "far0", "far1", "far2", "far3", "far4", "csent", "fsent"] + ["e%d" % _k for _k in range(140)]
 
 
 def rank_program(g, core, T, topo):
@@ -88,7 +23,8 @@ def rank_program(g, core, T, topo):
     if rank is None:
         return
     N = len(T.cores)
-    queues = {"G": g, "V": g.vector, "S": g.scalar, "P": g.tensor, "Y": g.sync}
+    vec, sca, pe = g.vector, g.scalar, g.tensor
+    queues = {"G": g, "V": vec, "S": sca, "P": pe, "Y": g.sync}
     known = {q: set() for q in queues}
     events = []
 
@@ -116,116 +52,126 @@ def rank_program(g, core, T, topo):
     def V(waits, fn, *a, **k):
         return run("V", waits, lambda: fn(*a), **k)
 
-    vec, sca, pe = g.vector, g.scalar, g.tensor
-    ts, tt = vec.tensor_scalar, vec.tensor_tensor
-    act = lambda waits, out, in_, func, **k: run("S", waits, lambda: sca.activation(out, in_, func, **k))
+    ts, tt, cp = vec.tensor_scalar, vec.tensor_tensor, vec.tensor_copy
+    act = lambda waits, out, in_, func, ev=None, **k: run("S", waits, lambda: sca.activation(out, in_, func, **k), ev=ev)
 
     def chain(waits, mms):
         use("P", waits)
         for m in mms:
             last = m()
-        e = event()
-        last.then_inc(e["sem"], 1)
-        e["total"] = 1
-        e["knows"] |= known["P"]
-        return e
+        return run("P", [], lambda: last)
 
     p = [T["p%d" % k] for k in range(8)]
 
     e_pos = run("Y", [], lambda: g.sync.dma_start(T.posi[0:8, :], T.pos[:, :]), inc=16)
-    e_tau = run("S", [], lambda: g.scalar.dma_start(T.taus[:, :], T.tau[:, :]), inc=16)
+    e_tau = run("S", [], lambda: sca.dma_start(T.taus[:, :], T.tau[:, :]), inc=16)
     e_tr = run("Y", [], lambda: g.sync.dma_start(T.trs[:, :], T.tr[:, :]), inc=16)
 
-    e_e8a = V([], vec.memset, T.e8a[0:8, :], -1.0)
-    e_onesf = V([], vec.memset, T.onesf[:, :], 1.0)
-    e_ones = V([], vec.memset, T.ones[:, :], 1.0)
-    e_one32 = V([], vec.memset, T.one32[:, :], 1.0)
-    e_m256 = V([], vec.memset, T.m256[:, :], 256.0)
-    e_wd0 = V([], vec.memset, T.wd[:, :], 0.0)
-
+    iota_i = lambda out, pat, base, cm: run("G", [], lambda: g.iota(out, pat, base, cm))
     iota_f = lambda out, pat, base: run("G", [], lambda: g.iota(out, pat, base, 0, allow_small_or_imprecise_dtypes=True))
-    sel = lambda waits, out, in_, pat, op, base, cm: run("G", waits, lambda: g.affine_select(out, in_, pat, op, 0.0, base, cm))
-    e_pcol = run("G", [], lambda: g.iota(T.pcol[:, 0:1], [[1, 1]], 0, 1))
-    e_e8b = sel([e_e8a], T.e8b[0:8, :], T.e8a[0:8, :], [[1, 128]], A.is_ge, 0, -16)
-    e_e8 = sel([e_e8b], T.e8[0:8, :], T.e8b[0:8, :], [[-1, 128]], A.is_ge, 15, 16)
+    sel = lambda waits, out, in_, pat, op, base, cm, ev=None: run("G", waits, lambda: g.affine_select(out, in_, pat, op, 0.0, base, cm), ev=ev)
+    e_pcol = iota_i(T.pcol[:, 0:1], [[1, 1]], 0, 1)
+    e_vi = iota_i(T.vi[:, :], [[1, 8], [16, 4], [0, 4]], 0, 0)
     e_yy = iota_f(T.yy[:, :], [[0, 16], [16, 16]], 8)
     e_xx = iota_f(T.xx[:, :], [[16, 16], [0, 16]], 8)
     e_yrow = iota_f(T.yrow[:, :], [[1, 256]], 0)
-    e_g16a = sel([e_onesf], T.g16a[:, :], T.onesf[:, :], [[-16, 8], [0, 16]], A.is_ge, 0, 1)
-    e_g16 = sel([e_g16a], T.g16[:, :], T.g16a[:, :], [[16, 8], [0, 16]], A.is_ge, 15, -1)
-    e_wdi = run("G", [], lambda: g.iota(T.wdi[:, :], [[1, 16]], 128, -1))
+    e_wdi = iota_i(T.wdi[:, :], [[1, 16]], 128, -1)
+    e_wfi = iota_i(T.wfi[:, :], [[1, 68]], 512 - 3, -4)
+    e_wd0 = V([], vec.memset, T.wd[:, :], 0.0)
+    e_ones = V([], vec.memset, T.ones[:, :], 1.0)
     e_ident = sel([e_ones], T.ident[:, :], T.ones[:, :], [[-1, 128]], A.is_equal, 0, 1)
-    e_wfi = run("G", [], lambda: g.iota(T.wfi[:, :], [[1, 136]], 1024 - 7, -8))
-    e_reset = sel([e_one32], T.reset[:, :], T.one32[:, :], [[0, 2], [1, 16]], A.not_equal, 0, 0)
-    e_mask8 = sel([e_m256], T.mask8[:, :], T.m256[:, :], [[-16, 8]], A.is_equal, 0, 1)
 
     e_r = V([e_pcol], ts, T.rcol[:, 0:1], T.pcol[:, 0:1], 15, None, A.bitwise_and)
+    e_pgi = V([], ts, T.pgi[:, 0:1], T.pcol[:, 0:1], 4, None, A.arith_shift_right)
+    e_pf = V([], cp, T.pf[:, 0:1], T.pcol[:, 0:1])
+    e_e8s = V([e_vi], ts, T.e8s[0:8, :], T.vi[0:8, :], 15, None, A.bitwise_and)
+    e_pgf = V([e_pgi], cp, T.pgf[:, 0:1], T.pgi[:, 0:1])
+    e_e8 = V([e_e8s, e_pf], ts, T.e8[0:8, :], T.e8s[0:8, :], T.pf[0:8, 0:1], -1.0, A.is_equal, A.mult)
     e_c16 = V([e_r], ts, T.c16[:, 0:1], T.rcol[:, 0:1], 16.0, 8.0, A.mult, A.add)
-    e_rm8 = V([e_r], ts, T.rm8[:, 0:1], T.rcol[:, 0:1], -8.0, None, A.add)
-    e_hcol = V([e_r], ts, T.hcol[:, 0:1], T.rcol[:, 0:1], -1.0, -4095.5 / 8192, A.mult, A.add)
+    e_rf = V([], cp, T.rf[:, 0:1], T.rcol[:, 0:1])
+    e_rm8 = V([], ts, T.rm8[:, 0:1], T.rcol[:, 0:1], -8.0, None, A.add)
+    lq = [T.l0, T.l1, T.l2, T.l3]
+    e_l = event()
+    for q in range(4):
+        V([e_pgf], ts, lq[q][:, :], T.vi[:, :], 16.0 * q, T.pgf[:, 0:1], A.subtract, A.is_equal, ev=e_l)
 
-    e_posf = V([e_pos], vec.tensor_copy, T.posf[0:8, :], T.posi[0:8, :])
+    e_posf = V([e_pos], cp, T.posf[0:8, :], T.posi[0:8, :])
+    e_r4 = V([], ts, T.r4[:, 0:1], T.pcol[:, 0:1], 3, None, A.bitwise_and)
     e_pb = run("P", [e_e8, e_posf], lambda: pe.matmul(p[0][:, 0:2], T.e8[0:8, :], T.posf[0:8, :], start=True, stop=True))
-    root = 8192.0 ** -0.5
-    e_np = V([e_pb], vec.tensor_copy, T.negp[:, :], p[0][:, 0:2])
-    e_nps = V([e_np], ts, T.nps[:, :], T.negp[:, :], root, None, A.mult)
+    e_np = V([e_pb], cp, T.negp[:, :], p[0][:, 0:2])
     nx, ny = T.negp[:, 0:1], T.negp[:, 1:2]
+    e_dyw = act([e_c16, e_np], T.dyw[:, 0:1], T.c16[:, 0:1], F.Square, bias=ny)
+    e_sy = act([e_yy], T.sy[:, :], T.yy[:, :], F.Square, bias=ny)
+    e_sx = act([e_xx], p[6][:, 0:256], T.xx[:, :], F.Square, bias=nx)
+
+    e_t1 = V([e_yy, e_np], ts, T.t1[:, :], T.yy[:, 0:16], nx, None, A.add)
     e_bx = V([e_rm8], tt, T.bx[:, 0:1], T.rm8[:, 0:1], nx, A.add)
-
-    e_sw = act([e_yy, e_np], T.sw[:, :], T.yy[:, 0:16], F.Square, bias=nx)
-    e_dyw = act([e_c16], T.dyw[:, 0:1], T.c16[:, 0:1], F.Square, bias=ny)
-    e_dx2 = act([e_bx], T.dx2[:, :], T.yy[:, 0:16], F.Square, bias=T.bx[:, 0:1])
-    e_sx0 = act([e_xx, e_nps], T.sx0[:, :], T.xx[:, :], F.Square, bias=T.nps[:, 0:1], scale=root)
-    e_sy = act([], T.sy[:, :], T.yy[:, :], F.Square, bias=T.nps[:, 1:2], scale=root)
-    e_sx = act([e_sx0, e_hcol], T.sx[:, :], T.sx0[:, :], F.Identity, bias=T.hcol[:, 0:1])
-    e_dy2 = act([e_yrow], T.dy2[:, :], T.yrow[:, :], F.Square, bias=ny)
-
+    e_sw = V([e_t1], tt, T.sw[:, :], T.t1[:, :], T.t1[:, :], A.mult)
     e_d2w = V([e_sw, e_dyw], ts, T.d2w[:, :], T.sw[:, :], T.dyw[:, 0:1], None, A.add)
     e_lo32 = V([e_d2w], ts, T.lo32[:, :], T.d2w[:, :], 5, 255, A.arith_shift_right, A.bitwise_and)
-    e_lo = V([e_lo32], vec.tensor_copy, T.lo[:, :], T.lo32[:, :])
-    e_dxs = V([e_dx2], ts, T.dxs[:, :], T.dx2[:, :], -15.5, 1.0 / 32, A.add, A.mult)
-    e_dg = V([e_xx, e_c16], ts, T.dg[:, :], T.xx[:, :], T.c16[:, 0:1], None, A.is_equal)
-    e_hd = V([e_sx, e_sy], tt, T.hd[:, :], T.sx[:, :], T.sy[:, :], A.add)
-    e_hm = V([e_hd], ts, T.hm[:, :], T.hd[:, :], 0.0, None, A.is_equal)
-    e_prod = V([e_hm, e_lo, e_tau], lambda: tt(T.prod[:, :], T.taus[:, :].indirect(T.lo[:, :]), T.hm[:, :], A.mult))
-    e_s = run("P", [e_prod, e_g16], lambda: pe.matmul(p[1][:, 0:256], T.g16[:, :], T.prod[:, :], start=True, stop=True))
+    e_lo = V([e_lo32], cp, T.lo[:, :], T.lo32[:, :])
+    e_d2i = V([e_sx, e_sy], tt, T.d2i[:, :], p[6][:, 0:256], T.sy[:, :], A.add)
+    e_hi = V([e_d2i], ts, T.hi[:, :], T.d2i[:, :], 13, None, A.arith_shift_right)
+    e_hm = V([e_hi, e_rf], ts, T.hm[:, :], T.hi[:, :], T.rf[:, 0:1], None, A.is_equal)
+    e_prod = [V([e_hm, e_lo, e_tau], lambda k=k: tt(T.prod[:, 128 * k:128 * k + 128], T.taus[:, :].indirect(T.lo[:, 8 * k:8 * k + 8]),
+                                                    T.hm[:, 128 * k:128 * k + 128], A.mult)) for k in range(2)]
+    for q in range(4):
+        use("P", [e_prod[q // 2], e_l])
+        mm = pe.matmul(p[1][:, 0:64], lq[q][:, :], T.prod[:, 64 * q:64 * q + 64], start=q == 0, stop=q == 3)
+    e_s = run("P", [], lambda: mm)
 
+    e_dx2 = act([e_bx], T.dx2[:, :], T.yy[:, 0:16], F.Square, bias=T.bx[:, 0:1])
+    e_dy2 = act([e_yrow], T.dy2[:, :], T.yrow[:, :], F.Square, bias=ny)
+    e_dxs = act([e_dx2], T.dxs[:, :], T.dx2[:, :], F.Copy, bias=-15.5 / 32, scale=1.0 / 32)
+    e_c4 = V([e_r4], ts, T.c4[:, 0:1], T.r4[:, 0:1], 16.0, 8.0, A.mult, A.add)
+    e_wdm = V([e_wdi], ts, T.wdm[:, :], T.wdi[:, :], 15, None, A.bitwise_and)
+    e_dg = V([e_xx, e_c4], ts, T.dg[:, :], T.xx[:, 0:64], T.c4[:, 0:1], None, A.is_equal)
+    e_wd = V([e_wdm, e_wd0], ts, T.wd[:, 16:32], T.wdm[:, :], 0.0, None, A.is_equal)
     e_jv, e_ja = event(), event()
-    NJ = 3
 
-    def table(q, a):
+    def table(a):
         o = T.jt[:, 256 * a:256 * a + 256]
-        if q == "V":
+        if a < 2:
             V([e_dxs, e_dy2], ts, o, T.dy2[:, :], 1.0 / 32, T.dxs[:, a:a + 1], A.mult, A.add, ev=e_jv)
         else:
-            run("S", [e_dxs, e_dy2], lambda: sca.activation(o, T.dy2[:, :], F.Identity, bias=T.dxs[:, a:a + 1], scale=1.0 / 32), ev=e_ja)
+            act([e_dxs, e_dy2], o, T.dy2[:, :], F.Identity, bias=T.dxs[:, a:a + 1], scale=1.0 / 32, ev=e_ja)
 
-    for a in range(NJ):
-        table("V", a)
-    for a in range(NJ, 16):
-        table("S", a)
-    e_dd = V([e_s, e_dg], tt, T.dd[:, :], p[1][:, 0:256], T.dg[:, :], A.mult)
-    e_t, src, n = e_dd, T.dd, 256
-    for dst in (T.a1, T.a2, T.a3, T.a4):
-        n //= 2
-        e_t = V([e_t], tt, dst[:, :], src[:, 0:n], src[:, n:2 * n], A.add)
-        src = dst
-    e_nl = V([e_t], vec.tensor_copy, T.nl[:, :], T.a4[:, :])
-    e_wdm = V([e_wdi], ts, T.wdm[:, :], T.wdi[:, :], 15, None, A.bitwise_and)
-    e_wd = V([e_wdm, e_wd0], ts, T.wd[:, 112:128], T.wdm[:, :], 0.0, None, A.is_equal)
-    e_tauo = V([e_tau], vec.tensor_copy, T.tauo[:, :], T.taus[:, :])
-    e_base = V([e_yy, e_rm8], ts, T.base[:, :], T.yy[:, 0:16], T.rm8[:, 0:1], None, A.add)
-    e_wc = V([e_yy], ts, T.wc[0:1, :], T.yy[0:1, 0:16], -8.0, 15.9375 / 16, A.add, A.mult)
-    e_wfm = V([e_wfi], ts, T.wfm[:, :], T.wfi[:, :], 127, None, A.bitwise_and)
-    e_wf = V([e_wfm], ts, T.wf[:, :], T.wfm[:, :], 0.0, None, A.is_equal)
+    for a in range(2, 11):
+        table(a)
+    e_dd = V([e_s, e_dg], tt, T.dd[:, :], p[1][:, 0:64], T.dg[:, :], A.mult)
+    e_a3 = V([e_dd], tt, T.a3[:, :], T.dd[:, 0:32], T.dd[:, 32:64], A.add)
+    e_a4 = V([e_a3], tt, T.a4[:, :], T.a3[:, 0:16], T.a3[:, 16:32], A.add)
+    e_nl = V([e_a4], cp, T.nl[:, :], T.a4[:, :])
 
-    e_vc = act([e_tr, e_nl], T.vc[:, :], T.trs[:, :].indirect(T.nl[:, :]), F.Copy)
-    e_cs = chain([e_vc, e_wd], [lambda k=k: pe.matmul(p[2][:, 0:32], T.wd[:, 112 - 16 * k:240 - 16 * k], T.vc[:, 32 * k:32 * k + 32],
-                                                      start=k == 0, stop=k == 7) for k in range(8)])
+    def along(q, c0, c1):
+        o, i = T.comp[:, 16 * c0:16 * c1], T.trs[:, :].indirect(T.tauo[:, c0:c1])
+        return V([e_tr, e_tauo], lambda: cp(o, i)) if q == "V" else act([e_tr, e_tauo], o, i, F.Copy)
+
+    h1 = 128
+    e_va = act([e_tr, e_nl], T.vc[:, 0:128], T.trs[:, :].indirect(T.nl[:, 0:8]), F.Copy)
+    e_vv = V([e_tr, e_nl], lambda: cp(T.vc[:, 128:256], T.trs[:, :].indirect(T.nl[:, 8:16])))
+    for a in range(11, 16):
+        table(a)
+    e_tauo = V([e_tau], cp, T.tauo[:, :], T.taus[:, :])
+    use("P", [e_vv, e_va, e_wd])
+    for k in range(8):
+        o = 32 * (k // 2)
+        mm = pe.matmul(p[2][o:o + 32, 0:32], T.wd[:, 16 - 16 * (k % 2):48 - 16 * (k % 2)], T.vc[:, 32 * k:32 * k + 32], start=k % 2 == 0, stop=k % 2 == 1)
+    e_cs = run("P", [], lambda: mm)
     own = slice(32 * rank, 32 * rank + 32)
-    e_own = act([e_cs], T.cland[:, own], p[2][:, 0:32], F.Copy)
+    e_own = V([e_cs], cp, T.cland[:, own], p[2][:, 0:32])
+    e_one32 = V([], vec.memset, T.one32[:, :], 1.0)
+    e_m256 = V([], vec.memset, T.m256[:, :], 256.0)
+    e_base = event()
+    for k in (0, 16):
+        V([e_yy, e_rm8], ts, T.base[:, k:k + 16], T.yy[:, 0:16], T.rm8[:, 0:1], None, A.add, ev=e_base)
+    e_c1 = along("V", 0, h1)
+    e_c2 = along("S", h1, 256)
+    table(0)
+    table(1)
 
-    others = [(rank + 1 + t) % N for t in range(N - 1)]
+    order = [(rank + 1 + t) % N for t in range(N)]
+    others = order[:-1]
 
     def dst_id(q):
         rid, pid, _ = topo.addr(T.cores[q])
@@ -241,119 +187,125 @@ def rank_program(g, core, T, topo):
     use("G", [e_own])
     g.remote_dma_fused([RemoteDMATransfer(dst_ids=[dst_id(q) for q in others], dma_engine_mask=bits(eng), remote_sem=T.sem.carr,
                                           srcs=[T.cland[:, own]], dsts=[T.cland[:, own] for q in others])], local_sem=T.sem.csent)
-    n_csent = len(eng)
+    e_reset = sel([e_one32], T.reset[:, :], T.one32[:, :], [[0, 2], [1, 16]], A.not_equal, 0, 0)
+    e_mask = event()
+    for k in (0, 8):
+        sel([e_m256], T.mask16[:, k:k + 8], T.m256[:, :], [[-1, 8]], A.is_equal, 0, 1, ev=e_mask)
 
-    h = 136
-    e_cv = V([e_tr, e_tauo], lambda: vec.tensor_copy(T.comp[:, 0:16 * h], T.trs[:, :].indirect(T.tauo[:, 0:h])))
-    e_ca = act([e_tr, e_tauo], T.comp[:, 16 * h:4096], T.trs[:, :].indirect(T.tauo[:, h:256]), F.Copy)
     e_nv, e_na = event(), event()
-    nv = 10
-    for r in range(nv):
-        V([e_cv, e_ca], vec.tensor_copy, T.nat[:, 256 * r:256 * r + 256], T.comp[:, r::16], ev=e_nv)
-    for r in range(nv, 16):
-        run("S", [e_cv, e_ca], lambda: sca.activation(T.nat[:, 256 * r:256 * r + 256], T.comp[:, r::16], F.Copy), ev=e_na)
+    for r in range(16):
+        o, i = T.nat[:, 256 * r:256 * r + 256], T.comp[:, r::16]
+        if r < 10:
+            V([e_c1, e_c2], cp, o, i, ev=e_nv)
+        else:
+            act([e_c1, e_c2], o, i, F.Copy, ev=e_na)
 
     use("P", [e_own, e_ident, e_base, e_ones])
-    pe.matmul(p[5][:, 0:16], T.ident[:, :], T.base[:, :], start=True, stop=False)
+    k0 = 2 * (rank + 1)
+    pe.matmul(p[5][:, 0:16], T.ident[:, :], T.base[:, k0:k0 + 16], start=True, stop=False)
     pe.matmul(p[3][:, 0:32], T.ident[:, :], T.cland[:, own], start=True, stop=False)
     pe.wait_ge(T.sem.carr, (N - 1) * len(eng))
     e_tot = chain([], [lambda i=i, q=q: pe.matmul(p[3][:, 0:32], T.ident[:, :], T.cland[:, 32 * q:32 * q + 32], start=False, stop=i == N - 2)
                        for i, q in enumerate(others)])
     e_sq = act([e_tot], T.sq[:, :], p[3][:, 0:32], F.Square)
-    e_e = chain([e_sq, e_g16], [lambda: pe.matmul(p[4][:, 0:32], T.g16[:, :], T.sq[:, :], start=True, stop=True)])
-    e_run = V([e_e, e_reset], vec.tensor_tensor_scan, T.run[:, :], T.reset[:, :], p[4][:, 0:32], 0.0, A.mult, A.max)
+    e_e = chain([e_sq, e_l], [lambda: pe.matmul(p[4][0:8, 0:32], T.l0[:, 0::16], T.sq[:, :], start=True, stop=True)])
+    e_run = V([e_e, e_reset], vec.tensor_tensor_scan, T.run[0:8, :], T.reset[0:8, :], p[4][0:8, 0:32], 0.0, A.mult, A.max)
     e_r2 = []
     for b in range(2):
-        e_a = act([e_run], T.lt[:, 16 * b:16 * b + 16], T.run[:, 16 * b:16 * b + 16], F.Sign, bias=T.run[:, 16 * b + 15:16 * b + 16], scale=-1.0,
-                  accum_out=T.acol[:, 4 * b:4 * b + 1])
-        e_r2.append(V([e_a, e_mask8], ts, T.rr[:, b::2], T.mask8[:, :], T.acol[:, 4 * b:4 * b + 1], None, A.mult))
-    e_off = chain(e_r2, [lambda: pe.matmul(p[5][:, 0:16], T.ones[:, :], T.rr[:, :], start=False, stop=True)])
-    e_offu = V([e_off], vec.tensor_copy, T.offu[:, :], p[5][:, 0:16])
+        e_a = act([e_run], T.lt[0:8, 16 * b:16 * b + 16], T.run[0:8, 16 * b:16 * b + 16], F.Sign, bias=T.run[0:8, 16 * b + 15:16 * b + 16], scale=-1.0,
+                  accum_out=T.acol[0:8, 4 * b:4 * b + 1])
+        e_r2.append(V([e_a, e_mask], ts, T.rr[0:8, b::2], T.mask16[0:8, rank + 1:rank + 9], T.acol[0:8, 4 * b:4 * b + 1], None, A.mult))
+    e_off = chain(e_r2, [lambda: pe.matmul(p[5][:, 0:16], T.ones[0:8, :], T.rr[0:8, :], start=False, stop=True)])
+    e_offu = V([e_off], cp, T.offu[:, :], p[5][:, 0:16])
 
-    def select(q0, q1):
-        return V([e_offu, e_jv, e_ja], lambda: vec.tensor_copy(T.flist[:, 32 * q0:32 * q1], T.jt[:, :].indirect(T.offu[:, 2 * q0:2 * q1])))
+    def select(t0, t1):
+        return V([e_offu, e_jv, e_ja], lambda: cp(T.flist[:, 32 * t0:32 * t1], T.jt[:, :].indirect(T.offu[:, 2 * t0:2 * t1])))
 
-    order = others + [rank]
-    e_sel = {}
-    bank = [0, 1, 2, 3, 4, 6, 7]
-    e_f = {}
+    groups = [[0], [1], [2, 3], [4, 5], [6]]
+    banks = [p[0], p[1], p[2], p[3], p[4]]
+    at = {t: (k, tts.index(t)) for k, tts in enumerate(groups) for t in tts}
+    e_f = {t: [] for t in range(N)}
 
-    def gather(t):
-        q = order[t]
-        o = 512 * q
-        e1 = V([e_sel[q], e_na, e_nv], lambda: vec.tensor_copy(T.ff[:, o:o + 256], T.nat[:, :].indirect(T.flist[:, 32 * q:32 * q + 16])))
-        e2 = act([e_sel[q], e_nv, e_na], T.ff[:, o + 256:o + 512], T.nat[:, :].indirect(T.flist[:, 32 * q + 16:32 * q + 32]), F.Copy)
-        e_f[t] = (e1, e2)
+    def gather(q, t, j0=0, j1=512):
+        o = T.ff[:, 512 * t + j0:512 * t + j1]
+        i = T.nat[:, :].indirect(T.flist[:, 32 * t + j0 // 16:32 * t + j1 // 16])
+        w = [e_nv, e_na, e_sel[t >= 2]]
+        e_f[t].append((j0, V(w, lambda: cp(o, i)) if q == "V" else act(w, o, i, F.Copy)))
 
     e_pt = {}
 
     def sensors(t):
-        q = order[t]
-        out = p[5] if t == 7 else p[bank[t]]
-        use("P", [e_f[t][0], e_wf])
-        for c in range(8):
-            if c == 4:
-                use("P", [e_f[t][1]])
-            mm = pe.matmul(out[:, 0:64], T.wf[:, 7 - c:135 - c], T.ff[:, 512 * q + 64 * c:512 * q + 64 * c + 64], start=c == 0, stop=t < 7 and c == 7)
-        if t < 7:
-            e_pt[t] = chain([], [lambda: mm])
+        for c in range(4):
+            use("P", [e for j0, e in e_f[t] if j0 < 128 * c + 128] + [e_wd])
+            f = T.ff[:, 512 * t + 128 * c:512 * t + 128 * c + 128]
+            if t == N - 1:
+                use("P", [e_wf])
+                pe.matmul(p[5][0:64, 0:128], T.wf[:, 3 - c:67 - c], f, start=c == 0, stop=False)
+            else:
+                o = 64 * at[t][1]
+                mm = pe.matmul(banks[at[t][0]][:, o + c:o + 64:4], f, T.wd[:, 16:32], start=True, stop=True)
+        if t < N - 1:
+            e_pt[t] = run("P", [], lambda: mm)
 
-    e_cp = {}
-
-    def take(t, q):
-        o, i = T.fsend[:, 64 * t:64 * t + 64], p[bank[t]][:, 0:64]
-        if q == "V":
-            e_cp[t] = V([e_pt[t]], vec.tensor_copy, o, i)
-        else:
-            e_cp[t] = act([e_pt[t]], o, i, F.Copy)
-
-    def send(tt_, k):
-        use("G", [e_cp[t] for t in tt_])
-        n = len(eng) // len(tt_)
-        own_f = slice(64 * rank, 64 * rank + 64)
+    def send(q, k):
+        tts = groups[k]
+        o, i = T.fsend[:, 64 * tts[0]:64 * tts[-1] + 64], banks[k][:, 0:64 * len(tts)]
+        w = [e_pt[t] for t in tts]
+        e = V(w, cp, o, i) if q == "V" else act(w, o, i, F.Copy)
+        use("G", [e])
+        n = len(eng) // len(tts)
         g.remote_dma_fused([RemoteDMATransfer(dst_ids=[dst_id(order[t])], dma_engine_mask=bits(eng[n * i:n * i + n]), remote_sem=T.sem["far%d" % k],
-                                              srcs=[T.fsend[:, 64 * t:64 * t + 64]], dsts=[T.fland[:, own_f]]) for i, t in enumerate(tt_)],
-                           local_sem=T.sem.fsent)
+                                              srcs=[T.fsend[:, 64 * t:64 * t + 64]], dsts=[T.fland[:, 64 * rank:64 * rank + 64]])
+                            for i, t in enumerate(tts)], local_sem=T.sem.fsent)
 
-    groups = [[0], [1, 2], [3, 4], [5, 6]]
-    for t in (0, 1):
-        e_sel[order[t]] = select(order[t], order[t] + 1)
-    gather(0)
+    e_sel = [select(0, 2)]
+    gather("V", 0, 0, 256)
+    gather("S", 0, 256, 512)
     sensors(0)
-    gather(1)
+    e_sel.append(select(2, N))
+    gather("S", 1, 256, 512)
+    send("V", 0)
+    gather("V", 1, 0, 256)
     sensors(1)
-    runs = []
-    for q in order[2:]:
-        if runs and runs[-1][1] == q:
-            runs[-1][1] = q + 1
-        else:
-            runs.append([q, q + 1])
-    for q0, q1 in runs:
-        e = select(q0, q1)
-        for q in range(q0, q1):
-            e_sel[q] = e
-    take(0, "S")
-    send([0], 0)
-    for t in range(2, 8):
-        gather(t)
-        sensors(t)
-        take(t - 1, "V" if t % 2 else "S")
-        if t % 2:
-            send(groups[t // 2], t // 2)
+    gather("S", 2)
+    sensors(2)
+    send("S", 1)
+    gather("V", 3)
+    sensors(3)
+    gather("S", 4)
+    sensors(4)
+    gather("V", 5, 0, 256)
+    gather("S", 5, 256, 512)
+    sensors(5)
+    send("V", 2)
+    gather("V", 6, 0, 320)
+    gather("S", 6, 320, 512)
+    sensors(6)
+    send("V", 3)
+    send("V", 4)
+    e_wfm = V([e_wfi], ts, T.wfm[:, :], T.wfi[:, :], 63, None, A.bitwise_and)
+    gather("V", 7, 0, 256)
+    gather("S", 7, 256, 512)
+    e_wf = V([e_wfm], ts, T.wf[:, :], T.wfm[:, :], 0.0, None, A.is_equal)
+    sensors(7)
+    e_wc = V([e_yy], ts, T.wc[0:1, :], T.yy[0:1, 0:16], -8.0, 15.9375 / 16, A.add, A.mult)
     e_w1 = V([e_offu], ts, T.w1[0:1, :], T.offu[0:1, :], 1.0 / 256, None, A.mult)
-    e_w2 = V([e_w1, e_wc], tt, T.w2[0:1, :], T.w1[0:1, :], T.wc[0:1, :], A.add)
+    e_w2, s = event(), k0 % 16
+    V([e_w1, e_wc], tt, T.w2[0:1, s:16], T.w1[0:1, 0:16 - s], T.wc[0:1, s:16], A.add, ev=e_w2)
+    if s:
+        V([], tt, T.w2[0:1, 0:s], T.w1[0:1, 16 - s:16], T.wc[0:1, 0:s], A.add, ev=e_w2)
     e_w = run("Y", [e_w2], lambda: g.sync.dma_start(T.w[:, :], T.w2[0:1, :]), inc=16)
 
-    for k, tt_ in enumerate(groups):
-        pe.wait_ge(T.sem["far%d" % k], len(eng))
-        for t in tt_:
+    for k, tts in enumerate(groups):
+        pe.wait_ge(T.sem["far%d" % k], len(eng) // len(tts) * len(tts))
+        for t in tts:
             q = (rank - 1 - t) % N
-            mm = pe.matmul(p[5][:, 0:64], T.ident[:, :], T.fland[:, 64 * q:64 * q + 64], start=False, stop=t == 6)
-    e_fin = chain([], [lambda: mm])
-    e_y = V([e_fin], vec.tensor_copy, T.ysb[:, :], p[5][:, 0:64])
-    e_st = run("Y", [e_y], lambda: g.sync.dma_start(T.y[:, :], T.ysb[:, :]), inc=16)
+            mm = pe.matmul(p[5][0:64, 0:128], T.fland[:, 64 * q:64 * q + 64], T.ident[:, :], start=False, stop=t == N - 2)
+    e_fin = run("P", [], lambda: mm)
+    e_y = V([e_fin], cp, T.ysb[0:64, :], p[5][0:64, 0:128])
+    e_st = run("Y", [e_y], lambda: g.sync.dma_start(T.y[:, :], T.ysb[0:64, :]), inc=16)
     use("Y", [e_w, e_st])
-    g.wait_ge(T.sem.csent, n_csent)
+    g.wait_ge(T.sem.csent, len(eng))
     g.wait_ge(T.sem.fsent, len(groups) * len(eng))
     for e in events:
         if not e["used"]:

@@ -3,19 +3,19 @@ from concourse.mybir import AluOpType as A, ActivationFunctionType as F
 
 _SB = {
     "int32": "posi 2 taus 256 vi 128 e8s 128 pgi 2 wdi 16 wdm 16 wfi 68 wfm 68 pcol 2 rcol 2 r4 2 d2w 16 lo32 16 d2i 256 hi 256",
-    "uint16": "tauo 256 lo 16 nl 16 offu 16 flist 256",
-    "bfloat16": "posf 2 trs 8192 comp 4096 nat 4096 e8 128 ones 128 ident 128 wd 144 wf 68 vc 256 cland 256 rr 16 base 32 "
-                "ff 4096 fsend 448 fland 512",
-    "float32": "negp 2 jt 4096 l0 128 l1 128 l2 128 l3 128 pgf 2 pf 2 rf 2 c16 2 c4 2 rm8 2 bx 2 dyw 2 yy 256 xx 256 yrow 256 sy 256 t1 16 sw 16 "
-               "hm 256 prod 256 dg 64 dd 64 a3 32 a4 16 dy2 256 dx2 16 dxs 16 sq 32 one32 32 reset 32 run 32 lt 32 acol 8 "
-               "m256 8 mask16 16 wc 16 w1 16 w2 16 ysb 128",
+    "uint16": "tauo 256 lo 16 nl 16 flist 256",
+    "bfloat16": "posf 2 trs 8192 comp 4096 nat 4096 e8 128 ones 256 ident 128 wd 144 wf 68 vc 256 cland 256 xq 16 lxa 128 lxb 128 em 256 "
+                "dga 256 dgb 256 ff 4096 fsend 448 fland 512",
+    "float32": "negp 2 lw 140 pgf 2 pf 2 rf 2 c16 2 c4 2 dyw 2 yy 256 xx 256 yrot 256 sy 256 t1 16 sw 16 "
+               "hm 256 prod 256 dg 64 dd 64 a3 32 a4 16 dy2 256 dy2s 256 dx2 2 dxs 2 rfree 128 le 32 identf 128 sq 32 "
+               "one16 16 run 16 lt 16 acol 2 wc 16 w2 16 ysb 128",
 }
 SCRATCH = {"p%d" % _k: ("psum", [128, 512], "float32") for _k in range(8)}
 for _d in _SB:
     _l = _SB[_d].split()
     for _k in range(0, len(_l), 2):
         SCRATCH[_l[_k]] = ("sbuf", [128, int(_l[_k + 1])], _d)
-SEMAPHORES = ["carr", "far0", "far1", "far2", "far3", "far4", "csent", "fsent"] + ["e%d" % _k for _k in range(140)]
+SEMAPHORES = ["carr%d" % _k for _k in range(8)] + ["far0", "far1", "far2", "far3", "far4", "csent", "fsent"] + ["e%d" % _k for _k in range(130)]
 
 
 def rank_program(g, core, T, topo):
@@ -67,19 +67,27 @@ def rank_program(g, core, T, topo):
     e_tau = run("S", [], lambda: sca.dma_start(T.taus[:, :], T.tau[:, :]), inc=16)
     e_tr = run("Y", [], lambda: g.sync.dma_start(T.trs[:, :], T.tr[:, :]), inc=16)
 
+    k0 = 2 * (rank + 1) % 16
     iota_i = lambda out, pat, base, cm: run("G", [], lambda: g.iota(out, pat, base, cm))
-    iota_f = lambda out, pat, base: run("G", [], lambda: g.iota(out, pat, base, 0, allow_small_or_imprecise_dtypes=True))
+    iota_f = lambda out, pat, base, ev=None: run("G", [], lambda: g.iota(out, pat, base, 0, allow_small_or_imprecise_dtypes=True), ev=ev)
     sel = lambda waits, out, in_, pat, op, base, cm, ev=None: run("G", waits, lambda: g.affine_select(out, in_, pat, op, 0.0, base, cm), ev=ev)
     e_pcol = iota_i(T.pcol[:, 0:1], [[1, 1]], 0, 1)
     e_vi = iota_i(T.vi[:, :], [[1, 8], [16, 4], [0, 4]], 0, 0)
     e_yy = iota_f(T.yy[:, :], [[0, 16], [16, 16]], 8)
     e_xx = iota_f(T.xx[:, :], [[16, 16], [0, 16]], 8)
-    e_yrow = iota_f(T.yrow[:, :], [[1, 256]], 0)
     e_wdi = iota_i(T.wdi[:, :], [[1, 16]], 128, -1)
-    e_wfi = iota_i(T.wfi[:, :], [[1, 68]], 512 - 3, -4)
-    e_wd0 = V([], vec.memset, T.wd[:, :], 0.0)
+    e_rfree = iota_f(T.rfree[0:16, :], [[0, 8], [1, 16]], 0)
+    e_yrot, e_em = event(), event()
+    n1 = 16 - k0
+    iota_f(T.yrot[:, 0:16 * n1], [[1, 16 * n1]], 16 * k0, ev=e_yrot)
+    if k0:
+        iota_f(T.yrot[:, 16 * n1:256], [[1, 16 * k0]], 0, ev=e_yrot)
     e_ones = V([], vec.memset, T.ones[:, :], 1.0)
-    e_ident = sel([e_ones], T.ident[:, :], T.ones[:, :], [[-1, 128]], A.is_equal, 0, 1)
+    e_wd0 = V([], vec.memset, T.wd[:, :], 0.0)
+    e_ident = sel([e_ones], T.ident[:, :], T.ones[:, 0:128], [[-1, 128]], A.is_equal, 0, 1)
+    sel([e_ones], T.em[0:16, 0:16 * n1], T.ones[0:16, 0:16 * n1], [[-1, n1], [0, 16]], A.is_equal, -k0, 1, ev=e_em)
+    if k0:
+        sel([], T.em[0:16, 16 * n1:256], T.ones[0:16, 16 * n1:256], [[-1, k0], [0, 16]], A.is_equal, 0, 1, ev=e_em)
 
     e_r = V([e_pcol], ts, T.rcol[:, 0:1], T.pcol[:, 0:1], 15, None, A.bitwise_and)
     e_pgi = V([], ts, T.pgi[:, 0:1], T.pcol[:, 0:1], 4, None, A.arith_shift_right)
@@ -88,25 +96,23 @@ def rank_program(g, core, T, topo):
     e_pgf = V([e_pgi], cp, T.pgf[:, 0:1], T.pgi[:, 0:1])
     e_e8 = V([e_e8s, e_pf], ts, T.e8[0:8, :], T.e8s[0:8, :], T.pf[0:8, 0:1], -1.0, A.is_equal, A.mult)
     e_c16 = V([e_r], ts, T.c16[:, 0:1], T.rcol[:, 0:1], 16.0, 8.0, A.mult, A.add)
-    e_rf = V([], cp, T.rf[:, 0:1], T.rcol[:, 0:1])
-    e_rm8 = V([], ts, T.rm8[:, 0:1], T.rcol[:, 0:1], -8.0, None, A.add)
-    lq = [T.l0, T.l1, T.l2, T.l3]
-    e_l = event()
-    for q in range(4):
-        V([e_pgf], ts, lq[q][:, :], T.vi[:, :], 16.0 * q, T.pgf[:, 0:1], A.subtract, A.is_equal, ev=e_l)
 
     e_posf = V([e_pos], cp, T.posf[0:8, :], T.posi[0:8, :])
-    e_r4 = V([], ts, T.r4[:, 0:1], T.pcol[:, 0:1], 3, None, A.bitwise_and)
     e_pb = run("P", [e_e8, e_posf], lambda: pe.matmul(p[0][:, 0:2], T.e8[0:8, :], T.posf[0:8, :], start=True, stop=True))
+    e_rf = V([e_r], cp, T.rf[:, 0:1], T.rcol[:, 0:1])
+    e_xq = V([e_posf, e_ones], ts, T.xq[0:8, :], T.ones[0:8, 0:16], T.posf[0:8, 0:1], None, A.mult)
     e_np = V([e_pb], cp, T.negp[:, :], p[0][:, 0:2])
     nx, ny = T.negp[:, 0:1], T.negp[:, 1:2]
     e_dyw = act([e_c16, e_np], T.dyw[:, 0:1], T.c16[:, 0:1], F.Square, bias=ny)
     e_sy = act([e_yy], T.sy[:, :], T.yy[:, :], F.Square, bias=ny)
     e_sx = act([e_xx], p[6][:, 0:256], T.xx[:, :], F.Square, bias=nx)
+    e_pq = run("P", [e_xq], lambda: pe.matmul(p[7][0:16, 0:128], T.xq[0:8, :], T.e8[0:8, :], start=True, stop=True))
 
     e_t1 = V([e_yy, e_np], ts, T.t1[:, :], T.yy[:, 0:16], nx, None, A.add)
-    e_bx = V([e_rm8], tt, T.bx[:, 0:1], T.rm8[:, 0:1], nx, A.add)
+    e_l = event()
+    V([], vec.memset, T.lw[:, 0:12], 0.0, ev=e_l)
     e_sw = V([e_t1], tt, T.sw[:, :], T.t1[:, :], T.t1[:, :], A.mult)
+    V([e_vi, e_pgf], ts, T.lw[:, 12:140], T.vi[:, :], T.pgf[:, 0:1], None, A.is_equal, ev=e_l)
     e_d2w = V([e_sw, e_dyw], ts, T.d2w[:, :], T.sw[:, :], T.dyw[:, 0:1], None, A.add)
     e_lo32 = V([e_d2w], ts, T.lo32[:, :], T.d2w[:, :], 5, 255, A.arith_shift_right, A.bitwise_and)
     e_lo = V([e_lo32], cp, T.lo[:, :], T.lo32[:, :])
@@ -117,58 +123,50 @@ def rank_program(g, core, T, topo):
                                                     T.hm[:, 128 * k:128 * k + 128], A.mult)) for k in range(2)]
     for q in range(4):
         use("P", [e_prod[q // 2], e_l])
-        mm = pe.matmul(p[1][:, 0:64], lq[q][:, :], T.prod[:, 64 * q:64 * q + 64], start=q == 0, stop=q == 3)
+        mm = pe.matmul(p[1][:, 0:64], T.lw[:, 12 - 4 * q:140 - 4 * q], T.prod[:, 64 * q:64 * q + 64], start=q == 0, stop=q == 3)
     e_s = run("P", [], lambda: mm)
 
-    e_dx2 = act([e_bx], T.dx2[:, :], T.yy[:, 0:16], F.Square, bias=T.bx[:, 0:1])
-    e_dy2 = act([e_yrow], T.dy2[:, :], T.yrow[:, :], F.Square, bias=ny)
-    e_dxs = act([e_dx2], T.dxs[:, :], T.dx2[:, :], F.Copy, bias=-15.5 / 32, scale=1.0 / 32)
-    e_c4 = V([e_r4], ts, T.c4[:, 0:1], T.r4[:, 0:1], 16.0, 8.0, A.mult, A.add)
+    e_dx2 = act([e_rf], T.dx2[:, 0:1], T.rf[:, 0:1], F.Square, bias=nx)
+    e_dy2 = act([e_yrot], T.dy2[:, :], T.yrot[:, :], F.Square, bias=ny)
+    e_dxs = act([e_dx2], T.dxs[:, 0:1], T.dx2[:, 0:1], F.Copy, bias=-15.5 / 32, scale=1.0 / 32)
+    e_dy2s = act([e_dxs, e_dy2], T.dy2s[:, :], T.dy2[:, :], F.Identity, bias=T.dxs[:, 0:1], scale=1.0 / 32)
+    e_idf = act([e_ident], T.identf[:, :], T.ident[:, :], F.Copy)
+    e_r4 = V([], ts, T.r4[:, 0:1], T.pcol[:, 0:1], 3, None, A.bitwise_and)
     e_wdm = V([e_wdi], ts, T.wdm[:, :], T.wdi[:, :], 15, None, A.bitwise_and)
-    e_dg = V([e_xx, e_c4], ts, T.dg[:, :], T.xx[:, 0:64], T.c4[:, 0:1], None, A.is_equal)
+    e_c4 = V([e_r4], ts, T.c4[:, 0:1], T.r4[:, 0:1], 16.0, 8.0, A.mult, A.add)
     e_wd = V([e_wdm, e_wd0], ts, T.wd[:, 16:32], T.wdm[:, :], 0.0, None, A.is_equal)
-    e_jv, e_ja = event(), event()
-
-    def table(a):
-        o = T.jt[:, 256 * a:256 * a + 256]
-        if a < 2:
-            V([e_dxs, e_dy2], ts, o, T.dy2[:, :], 1.0 / 32, T.dxs[:, a:a + 1], A.mult, A.add, ev=e_jv)
-        else:
-            act([e_dxs, e_dy2], o, T.dy2[:, :], F.Identity, bias=T.dxs[:, a:a + 1], scale=1.0 / 32, ev=e_ja)
-
-    for a in range(2, 11):
-        table(a)
+    e_dg = V([e_xx, e_c4], ts, T.dg[:, :], T.xx[:, 0:64], T.c4[:, 0:1], None, A.is_equal)
+    e_tauo = V([e_tau], cp, T.tauo[:, :], T.taus[:, :])
     e_dd = V([e_s, e_dg], tt, T.dd[:, :], p[1][:, 0:64], T.dg[:, :], A.mult)
     e_a3 = V([e_dd], tt, T.a3[:, :], T.dd[:, 0:32], T.dd[:, 32:64], A.add)
     e_a4 = V([e_a3], tt, T.a4[:, :], T.a3[:, 0:16], T.a3[:, 16:32], A.add)
     e_nl = V([e_a4], cp, T.nl[:, :], T.a4[:, :])
+    e_le0 = V([], vec.memset, T.le[:, :], 0.0)
+    e_le = event()
+    for h in range(2):
+        sel([e_l, e_le0], T.le[:, 17 * h:17 * h + 15:2], T.lw[:, 12:140:16], [[0, 8]], A.is_equal, 0, 0, ev=e_le)
+    e_wfi = iota_i(T.wfi[:, :], [[1, 68]], 512 - 3, -4)
+    e_wc = iota_f(T.wc[0:1, :], [[16, 16]], 0)
 
-    def along(q, c0, c1):
-        o, i = T.comp[:, 16 * c0:16 * c1], T.trs[:, :].indirect(T.tauo[:, c0:c1])
-        return V([e_tr, e_tauo], lambda: cp(o, i)) if q == "V" else act([e_tr, e_tauo], o, i, F.Copy)
-
-    h1 = 128
-    e_va = act([e_tr, e_nl], T.vc[:, 0:128], T.trs[:, :].indirect(T.nl[:, 0:8]), F.Copy)
-    e_vv = V([e_tr, e_nl], lambda: cp(T.vc[:, 128:256], T.trs[:, :].indirect(T.nl[:, 8:16])))
-    for a in range(11, 16):
-        table(a)
-    e_tauo = V([e_tau], cp, T.tauo[:, :], T.taus[:, :])
-    use("P", [e_vv, e_va, e_wd])
-    for k in range(8):
+    e_va = [act([e_tr, e_nl], T.vc[:, 64 * k:64 * k + 64], T.trs[:, :].indirect(T.nl[:, 4 * k:4 * k + 4]), F.Copy) for k in (0, 1)]
+    e_vv = [V([e_tr, e_nl], cp, T.vc[:, 64 * k:64 * k + 64], T.trs[:, :].indirect(T.nl[:, 4 * k:4 * k + 4])) for k in (2, 3)]
+    e_lxa = V([e_pq, e_rfree], tt, T.lxa[0:16, :], p[7][0:16, 0:128], T.rfree[0:16, :], A.add)
+    e_lxb = V([], vec.memset, T.lxb[0:16, :], 8.0)
+    use("P", [e_wd])
+    for k in (0, 1, 4, 5, 2, 3, 6, 7):
+        use("P", [(e_va + e_vv)[k // 2]])
         o = 32 * (k // 2)
         mm = pe.matmul(p[2][o:o + 32, 0:32], T.wd[:, 16 - 16 * (k % 2):48 - 16 * (k % 2)], T.vc[:, 32 * k:32 * k + 32], start=k % 2 == 0, stop=k % 2 == 1)
     e_cs = run("P", [], lambda: mm)
     own = slice(32 * rank, 32 * rank + 32)
     e_own = V([e_cs], cp, T.cland[:, own], p[2][:, 0:32])
-    e_one32 = V([], vec.memset, T.one32[:, :], 1.0)
-    e_m256 = V([], vec.memset, T.m256[:, :], 256.0)
-    e_base = event()
-    for k in (0, 16):
-        V([e_yy, e_rm8], ts, T.base[:, k:k + 16], T.yy[:, 0:16], T.rm8[:, 0:1], None, A.add, ev=e_base)
-    e_c1 = along("V", 0, h1)
-    e_c2 = along("S", h1, 256)
-    table(0)
-    table(1)
+    e_one16 = V([], vec.memset, T.one16[0:16, :], 1.0)
+
+    def along(q, c0, c1):
+        o, i = T.comp[:, 16 * c0:16 * c1], T.trs[:, :].indirect(T.tauo[:, c0:c1])
+        return V([e_tr, e_tauo], lambda: cp(o, i)) if q == "V" else act([e_tr, e_tauo], o, i, F.Copy)
+
+    e_c = [along("V", 0, 128), along("S", 128, 256)]
 
     order = [(rank + 1 + t) % N for t in range(N)]
     others = order[:-1]
@@ -185,41 +183,58 @@ def rank_program(g, core, T, topo):
 
     eng = [e for e in topo.engines(core, T.cores[others[0]]) if all(e in topo.engines(core, T.cores[q]) for q in others)]
     use("G", [e_own])
-    g.remote_dma_fused([RemoteDMATransfer(dst_ids=[dst_id(q) for q in others], dma_engine_mask=bits(eng), remote_sem=T.sem.carr,
+    g.remote_dma_fused([RemoteDMATransfer(dst_ids=[dst_id(q) for q in others], dma_engine_mask=bits(eng), remote_sem=T.sem["carr%d" % rank],
                                           srcs=[T.cland[:, own]], dsts=[T.cland[:, own] for q in others])], local_sem=T.sem.csent)
-    e_reset = sel([e_one32], T.reset[:, :], T.one32[:, :], [[0, 2], [1, 16]], A.not_equal, 0, 0)
-    e_mask = event()
-    for k in (0, 8):
-        sel([e_m256], T.mask16[:, k:k + 8], T.m256[:, :], [[-1, 8]], A.is_equal, 0, 1, ev=e_mask)
 
-    e_nv, e_na = event(), event()
-    for r in range(16):
-        o, i = T.nat[:, 256 * r:256 * r + 256], T.comp[:, r::16]
-        if r < 10:
-            V([e_c1, e_c2], cp, o, i, ev=e_nv)
-        else:
-            act([e_c1, e_c2], o, i, F.Copy, ev=e_na)
+    e_n = {q: event() for q in "GVS"}
 
-    use("P", [e_own, e_ident, e_base, e_ones])
-    k0 = 2 * (rank + 1)
-    pe.matmul(p[5][:, 0:16], T.ident[:, :], T.base[:, k0:k0 + 16], start=True, stop=False)
+    def reorder(q, pieces):
+        for r, h in pieces:
+            o, i = T.nat[:, 256 * r + 128 * h:256 * r + 128 * h + 128], T.comp[:, 2048 * h + r:2048 * h + 2048:16]
+            if q == "G":
+                sel([e_c[h]], o, i, [[0, 128]], A.is_equal, 0, 0, ev=e_n[q])
+            elif q == "V":
+                V([e_c[h]], cp, o, i, ev=e_n[q])
+            else:
+                act([e_c[h]], o, i, F.Copy, ev=e_n[q])
+
+    pieces = [(r, h) for h in range(2) for r in range(16)]
+    reorder("G", pieces[27:])
+    reorder("S", pieces[18:27])
+    reorder("V", pieces[:18])
+
+    use("P", [e_own, e_ident])
     pe.matmul(p[3][:, 0:32], T.ident[:, :], T.cland[:, own], start=True, stop=False)
-    pe.wait_ge(T.sem.carr, (N - 1) * len(eng))
-    e_tot = chain([], [lambda i=i, q=q: pe.matmul(p[3][:, 0:32], T.ident[:, :], T.cland[:, 32 * q:32 * q + 32], start=False, stop=i == N - 2)
-                       for i, q in enumerate(others)])
+    parts = [(0, 64), (64, 256)]
+    use("P", [e_idf, e_dy2s, e_lxa])
+    for k, (c0, c1) in enumerate(parts):
+        pe.matmul(p[6 + k][:, 0:c1 - c0], T.identf[:, :], T.dy2s[:, c0:c1], start=True, stop=False)
+    for q in reversed(others):
+        pe.wait_ge(T.sem["carr%d" % q], len(eng))
+        mm = pe.matmul(p[3][:, 0:32], T.ident[:, :], T.cland[:, 32 * q:32 * q + 32], start=False, stop=q == others[0])
+    e_tot = run("P", [], lambda: mm)
     e_sq = act([e_tot], T.sq[:, :], p[3][:, 0:32], F.Square)
-    e_e = chain([e_sq, e_l], [lambda: pe.matmul(p[4][0:8, 0:32], T.l0[:, 0::16], T.sq[:, :], start=True, stop=True)])
-    e_run = V([e_e, e_reset], vec.tensor_tensor_scan, T.run[0:8, :], T.reset[0:8, :], p[4][0:8, 0:32], 0.0, A.mult, A.max)
-    e_r2 = []
-    for b in range(2):
-        e_a = act([e_run], T.lt[0:8, 16 * b:16 * b + 16], T.run[0:8, 16 * b:16 * b + 16], F.Sign, bias=T.run[0:8, 16 * b + 15:16 * b + 16], scale=-1.0,
-                  accum_out=T.acol[0:8, 4 * b:4 * b + 1])
-        e_r2.append(V([e_a, e_mask], ts, T.rr[0:8, b::2], T.mask16[0:8, rank + 1:rank + 9], T.acol[0:8, 4 * b:4 * b + 1], None, A.mult))
-    e_off = chain(e_r2, [lambda: pe.matmul(p[5][:, 0:16], T.ones[0:8, :], T.rr[0:8, :], start=False, stop=True)])
-    e_offu = V([e_off], cp, T.offu[:, :], p[5][:, 0:16])
+    e_e = chain([e_sq, e_le], [lambda: pe.matmul(p[4][0:16, 0:16], T.le[:, 0:16], T.sq[:, 0:16], start=True, stop=False),
+                               lambda: pe.matmul(p[4][0:16, 0:16], T.le[:, 16:32], T.sq[:, 16:32], start=False, stop=True)])
+    e_run = V([e_e, e_one16], vec.tensor_tensor_scan, T.run[0:16, :], T.one16[0:16, :], p[4][0:16, 0:16], 0.0, A.mult, A.max)
+    ac = T.acol[0:16, 0:1]
+    e_ac = act([e_run], T.lt[0:16, :], T.run[0:16, :], F.Sign, bias=T.run[0:16, 15:16], scale=-1.0, accum_out=ac)
+    e_d = []
+    for k, (c0, c1) in enumerate(parts):
+        e_a = V([e_ac, e_em], ts, T.dga[0:16, c0:c1], T.em[0:16, c0:c1], ac, None, A.mult)
+        e_b = V([], ts, T.dgb[0:16, c0:c1], T.em[0:16, c0:c1], ac, ac, A.mult, A.mult)
+        o = p[6 + k][:, 0:c1 - c0]
+        use("P", [e_a])
+        pe.matmul(o, T.lxa[0:16, :], T.dga[0:16, c0:c1], start=False, stop=False)
+        e_d.append(chain([e_b, e_lxb], [lambda: pe.matmul(o, T.lxb[0:16, :], T.dgb[0:16, c0:c1], start=False, stop=True)]))
 
-    def select(t0, t1):
-        return V([e_offu, e_jv, e_ja], lambda: cp(T.flist[:, 32 * t0:32 * t1], T.jt[:, :].indirect(T.offu[:, 2 * t0:2 * t1])))
+    e_sel = {}
+
+    def select(k):
+        t0, t1 = parts[k][0] // 32, parts[k][1] // 32
+        e = V([e_d[k]], cp, T.flist[:, 32 * t0:32 * t1], p[6 + k][:, 0:32 * (t1 - t0)])
+        for t in range(t0, t1):
+            e_sel[t] = e
 
     groups = [[0], [1], [2, 3], [4, 5], [6]]
     banks = [p[0], p[1], p[2], p[3], p[4]]
@@ -229,10 +244,16 @@ def rank_program(g, core, T, topo):
     def gather(q, t, j0=0, j1=512):
         o = T.ff[:, 512 * t + j0:512 * t + j1]
         i = T.nat[:, :].indirect(T.flist[:, 32 * t + j0 // 16:32 * t + j1 // 16])
-        w = [e_nv, e_na, e_sel[t >= 2]]
+        w = [e_n["G"], e_n["V"], e_n["S"], e_sel[t]]
         e_f[t].append((j0, V(w, lambda: cp(o, i)) if q == "V" else act(w, o, i, F.Copy)))
 
-    e_pt = {}
+    e_pt, last = {}, [None]
+
+    def collect(k):
+        pe.wait_ge(T.sem["far%d" % k], len(eng) // len(groups[k]) * len(groups[k]))
+        for t in groups[k]:
+            q = (rank - 1 - t) % N
+            last[0] = pe.matmul(p[5][0:64, 0:128], T.fland[:, 64 * q:64 * q + 64], T.ident[:, :], start=t == 0, stop=t == N - 2)
 
     def sensors(t):
         for c in range(4):
@@ -240,68 +261,65 @@ def rank_program(g, core, T, topo):
             f = T.ff[:, 512 * t + 128 * c:512 * t + 128 * c + 128]
             if t == N - 1:
                 use("P", [e_wf])
-                pe.matmul(p[5][0:64, 0:128], T.wf[:, 3 - c:67 - c], f, start=c == 0, stop=False)
+                pe.matmul(p[5][0:64, 0:128], T.wf[:, 3 - c:67 - c], f, start=False, stop=False)
             else:
                 o = 64 * at[t][1]
                 mm = pe.matmul(banks[at[t][0]][:, o + c:o + 64:4], f, T.wd[:, 16:32], start=True, stop=True)
         if t < N - 1:
             e_pt[t] = run("P", [], lambda: mm)
 
-    def send(q, k):
+    def send(k):
         tts = groups[k]
-        o, i = T.fsend[:, 64 * tts[0]:64 * tts[-1] + 64], banks[k][:, 0:64 * len(tts)]
-        w = [e_pt[t] for t in tts]
-        e = V(w, cp, o, i) if q == "V" else act(w, o, i, F.Copy)
+        e = V([e_pt[t] for t in tts], cp, T.fsend[:, 64 * tts[0]:64 * tts[-1] + 64], banks[k][:, 0:64 * len(tts)])
         use("G", [e])
         n = len(eng) // len(tts)
         g.remote_dma_fused([RemoteDMATransfer(dst_ids=[dst_id(order[t])], dma_engine_mask=bits(eng[n * i:n * i + n]), remote_sem=T.sem["far%d" % k],
                                               srcs=[T.fsend[:, 64 * t:64 * t + 64]], dsts=[T.fland[:, 64 * rank:64 * rank + 64]])
                             for i, t in enumerate(tts)], local_sem=T.sem.fsent)
 
-    e_sel = [select(0, 2)]
+    select(0)
     gather("V", 0, 0, 256)
     gather("S", 0, 256, 512)
     sensors(0)
-    e_sel.append(select(2, N))
-    gather("S", 1, 256, 512)
-    send("V", 0)
+    select(1)
     gather("V", 1, 0, 256)
+    gather("S", 1, 256, 512)
+    send(0)
     sensors(1)
     gather("S", 2)
     sensors(2)
-    send("S", 1)
     gather("V", 3)
+    send(1)
     sensors(3)
     gather("S", 4)
     sensors(4)
-    gather("V", 5, 0, 256)
-    gather("S", 5, 256, 512)
+    gather("V", 5, 0, 320)
+    send(2)
+    gather("S", 5, 320, 512)
     sensors(5)
-    send("V", 2)
-    gather("V", 6, 0, 320)
-    gather("S", 6, 320, 512)
+    gather("V", 6, 0, 256)
+    gather("S", 6, 256, 512)
+    send(3)
     sensors(6)
-    send("V", 3)
-    send("V", 4)
     e_wfm = V([e_wfi], ts, T.wfm[:, :], T.wfi[:, :], 63, None, A.bitwise_and)
-    gather("V", 7, 0, 256)
-    gather("S", 7, 256, 512)
     e_wf = V([e_wfm], ts, T.wf[:, :], T.wfm[:, :], 0.0, None, A.is_equal)
+    send(4)
+    gather("V", 7, 0, 128)
+    gather("S", 7, 128, 512)
+    use("P", [e_sel[0]])
+    mm = pe.matmul(p[6][0:1, k0:16], T.ones[0:16, 0:1], T.dga[0:16, 0:16 * n1:16], start=True, stop=True)
+    if k0:
+        mm = pe.matmul(p[6][0:1, 0:k0], T.ones[0:16, 0:1], T.dga[0:16, 16 * n1:256:16], start=True, stop=True)
+    e_w1 = run("P", [], lambda: mm)
+    collect(0)
+    collect(1)
     sensors(7)
-    e_wc = V([e_yy], ts, T.wc[0:1, :], T.yy[0:1, 0:16], -8.0, 15.9375 / 16, A.add, A.mult)
-    e_w1 = V([e_offu], ts, T.w1[0:1, :], T.offu[0:1, :], 1.0 / 256, None, A.mult)
-    e_w2, s = event(), k0 % 16
-    V([e_w1, e_wc], tt, T.w2[0:1, s:16], T.w1[0:1, 0:16 - s], T.wc[0:1, s:16], A.add, ev=e_w2)
-    if s:
-        V([], tt, T.w2[0:1, 0:s], T.w1[0:1, 16 - s:16], T.wc[0:1, 0:s], A.add, ev=e_w2)
+    e_w2 = V([e_w1, e_wc], tt, T.w2[0:1, :], p[6][0:1, 0:16], T.wc[0:1, :], A.add)
     e_w = run("Y", [e_w2], lambda: g.sync.dma_start(T.w[:, :], T.w2[0:1, :]), inc=16)
 
-    for k, tts in enumerate(groups):
-        pe.wait_ge(T.sem["far%d" % k], len(eng) // len(tts) * len(tts))
-        for t in tts:
-            q = (rank - 1 - t) % N
-            mm = pe.matmul(p[5][0:64, 0:128], T.fland[:, 64 * q:64 * q + 64], T.ident[:, :], start=False, stop=t == N - 2)
-    e_fin = run("P", [], lambda: mm)
+    for k in range(2, len(groups)):
+        collect(k)
+    e_fin = run("P", [], lambda: last[0])
     e_y = V([e_fin], cp, T.ysb[0:64, :], p[5][0:64, 0:128])
     e_st = run("Y", [e_y], lambda: g.sync.dma_start(T.y[:, :], T.ysb[0:64, :]), inc=16)
     use("Y", [e_w, e_st])

@@ -2,20 +2,20 @@ from concourse.bass import DstId, RemoteDMATransfer
 from concourse.mybir import AluOpType as A, ActivationFunctionType as F
 
 _SB = {
-    "int32": "posi 2 taus 256 vi 128 e8s 128 pgi 2 wdi 16 wdm 16 wfi 68 wfm 68 pcol 2 rcol 2 r4 2 d2w 16 lo32 16 d2i 256 hi 256",
+    "int32": "posi 2 taus 256 vi 128 e8s 128 pgi 2 wdi 16 wdm 16 pcol 2 rcol 2 r4 2 d2w 16 lo32 16 d2i 256 hi 256",
     "uint16": "tauo 256 lo 16 nl 16 flist 256",
-    "bfloat16": "posf 2 trs 8192 comp 4096 nat 4096 e8 128 ones 256 ident 128 wd 144 wf 68 vc 256 cland 256 xq 16 lxa 128 lxb 128 em 256 "
+    "bfloat16": "posf 2 trs 8192 nat 4096 e8 128 ones 256 ident 128 wd 144 wf 80 vc 256 cland 256 xq 16 lxa 128 lxb 128 em 256 "
                 "dga 256 dgb 256 ff 4096 fsend 448 fland 512",
     "float32": "negp 2 lw 140 pgf 2 pf 2 rf 2 c16 2 c4 2 dyw 2 yy 256 xx 256 yrot 256 sy 256 t1 16 sw 16 "
                "hm 256 prod 256 dg 64 dd 64 a3 32 a4 16 dy2 256 dy2s 256 dx2 2 dxs 2 rfree 128 le 32 identf 128 sq 32 "
-               "one16 16 run 16 lt 16 acol 2 wc 16 w2 16 ysb 128",
+               "one64 64 pw 260 tauf 256 taut 256 run 16 lt 16 acol 2 wc 16 w2 16 ysb 128",
 }
 SCRATCH = {"p%d" % _k: ("psum", [128, 512], "float32") for _k in range(8)}
 for _d in _SB:
     _l = _SB[_d].split()
     for _k in range(0, len(_l), 2):
         SCRATCH[_l[_k]] = ("sbuf", [128, int(_l[_k + 1])], _d)
-SEMAPHORES = ["carr%d" % _k for _k in range(8)] + ["far0", "far1", "far2", "far3", "far4", "csent", "fsent"] + ["e%d" % _k for _k in range(130)]
+SEMAPHORES = ["carr%d" % _k for _k in range(8)] + ["far%d" % _k for _k in range(5)] + ["csent", "fsent", "shared", "ssent"] + ["e%d" % _k for _k in range(130)]
 
 
 def rank_program(g, core, T, topo):
@@ -67,27 +67,54 @@ def rank_program(g, core, T, topo):
     e_tau = run("S", [], lambda: sca.dma_start(T.taus[:, :], T.tau[:, :]), inc=16)
     e_tr = run("Y", [], lambda: g.sync.dma_start(T.trs[:, :], T.tr[:, :]), inc=16)
 
-    k0 = 2 * (rank + 1) % 16
+    def kind(a, b):
+        a, b = topo.chip(T.cores[a]), topo.chip(T.cores[b])
+        return 2 if topo.mates(a, b) else 1 if topo.same_plane(a, b) else 0
+
+    def ordered(r):
+        return sorted([q for q in range(N) if q != r], key=lambda q: (kind(r, q), (q - r) % N)) + [r]
+
+    order = ordered(rank)
+    others, mate = order[:-1], order[-2]
+    senders = [[q for q in range(N) if ordered(q)[t] == rank][0] for t in range(N)]
+
+    def dst_id(q):
+        rid, pid, _ = topo.addr(T.cores[q])
+        return DstId(rid=rid, pnc=pid)
+
+    def bits(es):
+        m = 0
+        for e in es:
+            m |= 1 << e
+        return m
+
+    eng = [e for e in topo.engines(core, T.cores[mate]) if all(e in topo.engines(core, T.cores[q]) for q in others)]
+
+    runs, t = [], 0
+    while t < N:
+        n, d = 1, (order[t + 1] - order[t] if t + 1 < N else 1)
+        while t + n < N and order[t + n] == order[t] + n * d:
+            n += 1
+        runs.append((t, order[t], d, n))
+        t += n
+
     iota_i = lambda out, pat, base, cm: run("G", [], lambda: g.iota(out, pat, base, cm))
     iota_f = lambda out, pat, base, ev=None: run("G", [], lambda: g.iota(out, pat, base, 0, allow_small_or_imprecise_dtypes=True), ev=ev)
     sel = lambda waits, out, in_, pat, op, base, cm, ev=None: run("G", waits, lambda: g.affine_select(out, in_, pat, op, 0.0, base, cm), ev=ev)
+    e_one64 = V([], vec.memset, T.one64[:, :], 1.0)
+    e_ones = V([], vec.memset, T.ones[:, :], 1.0)
+    e_wd0 = V([], vec.memset, T.wd[:, :], 0.0)
+    e_pw0 = V([], vec.memset, T.pw[:, :], 0.0)
+    e_tab0 = V([], vec.memset, T.wf[:, :] if rank < mate else T.le[:, :], 0.0)
     e_pcol = iota_i(T.pcol[:, 0:1], [[1, 1]], 0, 1)
     e_vi = iota_i(T.vi[:, :], [[1, 8], [16, 4], [0, 4]], 0, 0)
     e_yy = iota_f(T.yy[:, :], [[0, 16], [16, 16]], 8)
     e_xx = iota_f(T.xx[:, :], [[16, 16], [0, 16]], 8)
+    e_pw = event()
+    for o in range(2):
+        sel([e_one64, e_pw0], T.pw[:, 130 * o + 1:130 * o + 129:2], T.one64[:, :], [[-32, 4], [-1, 16]], A.is_equal, -16 * o, 1, ev=e_pw)
     e_wdi = iota_i(T.wdi[:, :], [[1, 16]], 128, -1)
-    e_rfree = iota_f(T.rfree[0:16, :], [[0, 8], [1, 16]], 0)
-    e_yrot, e_em = event(), event()
-    n1 = 16 - k0
-    iota_f(T.yrot[:, 0:16 * n1], [[1, 16 * n1]], 16 * k0, ev=e_yrot)
-    if k0:
-        iota_f(T.yrot[:, 16 * n1:256], [[1, 16 * k0]], 0, ev=e_yrot)
-    e_ones = V([], vec.memset, T.ones[:, :], 1.0)
-    e_wd0 = V([], vec.memset, T.wd[:, :], 0.0)
     e_ident = sel([e_ones], T.ident[:, :], T.ones[:, 0:128], [[-1, 128]], A.is_equal, 0, 1)
-    sel([e_ones], T.em[0:16, 0:16 * n1], T.ones[0:16, 0:16 * n1], [[-1, n1], [0, 16]], A.is_equal, -k0, 1, ev=e_em)
-    if k0:
-        sel([], T.em[0:16, 16 * n1:256], T.ones[0:16, 16 * n1:256], [[-1, k0], [0, 16]], A.is_equal, 0, 1, ev=e_em)
 
     e_r = V([e_pcol], ts, T.rcol[:, 0:1], T.pcol[:, 0:1], 15, None, A.bitwise_and)
     e_pgi = V([], ts, T.pgi[:, 0:1], T.pcol[:, 0:1], 4, None, A.arith_shift_right)
@@ -114,10 +141,41 @@ def rank_program(g, core, T, topo):
     e_sw = V([e_t1], tt, T.sw[:, :], T.t1[:, :], T.t1[:, :], A.mult)
     V([e_vi, e_pgf], ts, T.lw[:, 12:140], T.vi[:, :], T.pgf[:, 0:1], None, A.is_equal, ev=e_l)
     e_d2w = V([e_sw, e_dyw], ts, T.d2w[:, :], T.sw[:, :], T.dyw[:, 0:1], None, A.add)
+
+    e_tauf = V([e_tau], cp, T.tauf[:, :], T.taus[:, :])
+
+    def pairs(o):
+        use("P", [e_tauf, e_pw])
+        for x in range(2):
+            mm = pe.matmul(p[5][:, 128 * o:128 * o + 128], T.pw[:, 130 * o + 1 - x:130 * o + 129 - x], T.tauf[:, 128 * x:128 * x + 128],
+                           start=x == 0, stop=x == 1)
+        return run("P", [], lambda: mm)
+
+    pairs(0)
     e_lo32 = V([e_d2w], ts, T.lo32[:, :], T.d2w[:, :], 5, 255, A.arith_shift_right, A.bitwise_and)
     e_lo = V([e_lo32], cp, T.lo[:, :], T.lo32[:, :])
+    e_wdm = V([e_wdi], ts, T.wdm[:, :], T.wdi[:, :], 15, None, A.bitwise_and)
     e_d2i = V([e_sx, e_sy], tt, T.d2i[:, :], p[6][:, 0:256], T.sy[:, :], A.add)
     e_hi = V([e_d2i], ts, T.hi[:, :], T.d2i[:, :], 13, None, A.arith_shift_right)
+
+    e_shared = {"n": len(events), "sem": T.sem.shared, "total": len(eng), "knows": set(), "used": False}
+    events.append(e_shared)
+    if rank < mate:
+        e_made = V([e_wdm, e_tab0], ts, T.wf[:, 3:67:4], T.wdm[:, :], 0.0, None, A.is_equal)
+        e_wf, e_le, table = e_made, e_shared, T.wf
+    else:
+        e_made = event()
+        for h in range(2):
+            sel([e_l, e_tab0], T.le[:, 17 * h:17 * h + 15:2], T.lw[:, 12:140:16], [[0, 8]], A.is_equal, 0, 0, ev=e_made)
+        e_wf, e_le, table = e_shared, e_made, T.le
+    use("G", [e_made])
+    g.remote_dma_fused([RemoteDMATransfer(dst_ids=[dst_id(mate)], dma_engine_mask=bits(eng), remote_sem=T.sem.shared,
+                                          srcs=[table[:, :]], dsts=[table[:, :]])], local_sem=T.sem.ssent)
+    e_yrot = event()
+    for t, q, d, n in runs:
+        iota_f(T.yrot[:, 32 * t:32 * t + 32 * n], [[32 * d, n], [1, 32]], 32 * q, ev=e_yrot)
+    e_rfree = iota_f(T.rfree[0:16, :], [[0, 8], [1, 16]], 0)
+
     e_hm = V([e_hi, e_rf], ts, T.hm[:, :], T.hi[:, :], T.rf[:, 0:1], None, A.is_equal)
     e_prod = [V([e_hm, e_lo, e_tau], lambda k=k: tt(T.prod[:, 128 * k:128 * k + 128], T.taus[:, :].indirect(T.lo[:, 8 * k:8 * k + 8]),
                                                     T.hm[:, 128 * k:128 * k + 128], A.mult)) for k in range(2)]
@@ -125,28 +183,27 @@ def rank_program(g, core, T, topo):
         use("P", [e_prod[q // 2], e_l])
         mm = pe.matmul(p[1][:, 0:64], T.lw[:, 12 - 4 * q:140 - 4 * q], T.prod[:, 64 * q:64 * q + 64], start=q == 0, stop=q == 3)
     e_s = run("P", [], lambda: mm)
+    e_z = pairs(1)
 
     e_dx2 = act([e_rf], T.dx2[:, 0:1], T.rf[:, 0:1], F.Square, bias=nx)
-    e_dy2 = act([e_yrot], T.dy2[:, :], T.yrot[:, :], F.Square, bias=ny)
     e_dxs = act([e_dx2], T.dxs[:, 0:1], T.dx2[:, 0:1], F.Copy, bias=-15.5 / 32, scale=1.0 / 32)
-    e_dy2s = act([e_dxs, e_dy2], T.dy2s[:, :], T.dy2[:, :], F.Identity, bias=T.dxs[:, 0:1], scale=1.0 / 32)
     e_idf = act([e_ident], T.identf[:, :], T.ident[:, :], F.Copy)
+    e_dy2 = act([e_yrot], T.dy2[:, :], T.yrot[:, :], F.Square, bias=ny)
+    e_dy2s = act([e_dxs, e_dy2], T.dy2s[:, :], T.dy2[:, :], F.Identity, bias=T.dxs[:, 0:1], scale=1.0 / 32)
     e_r4 = V([], ts, T.r4[:, 0:1], T.pcol[:, 0:1], 3, None, A.bitwise_and)
-    e_wdm = V([e_wdi], ts, T.wdm[:, :], T.wdi[:, :], 15, None, A.bitwise_and)
-    e_c4 = V([e_r4], ts, T.c4[:, 0:1], T.r4[:, 0:1], 16.0, 8.0, A.mult, A.add)
     e_wd = V([e_wdm, e_wd0], ts, T.wd[:, 16:32], T.wdm[:, :], 0.0, None, A.is_equal)
+    e_c4 = V([e_r4], ts, T.c4[:, 0:1], T.r4[:, 0:1], 16.0, 8.0, A.mult, A.add)
     e_dg = V([e_xx, e_c4], ts, T.dg[:, :], T.xx[:, 0:64], T.c4[:, 0:1], None, A.is_equal)
-    e_tauo = V([e_tau], cp, T.tauo[:, :], T.taus[:, :])
     e_dd = V([e_s, e_dg], tt, T.dd[:, :], p[1][:, 0:64], T.dg[:, :], A.mult)
     e_a3 = V([e_dd], tt, T.a3[:, :], T.dd[:, 0:32], T.dd[:, 32:64], A.add)
     e_a4 = V([e_a3], tt, T.a4[:, :], T.a3[:, 0:16], T.a3[:, 16:32], A.add)
     e_nl = V([e_a4], cp, T.nl[:, :], T.a4[:, :])
-    e_le0 = V([], vec.memset, T.le[:, :], 0.0)
-    e_le = event()
-    for h in range(2):
-        sel([e_l, e_le0], T.le[:, 17 * h:17 * h + 15:2], T.lw[:, 12:140:16], [[0, 8]], A.is_equal, 0, 0, ev=e_le)
-    e_wfi = iota_i(T.wfi[:, :], [[1, 68]], 512 - 3, -4)
-    e_wc = iota_f(T.wc[0:1, :], [[16, 16]], 0)
+
+    e_tt, e_tauo = event(), [None, None]
+    for k in range(8):
+        V([e_z], vec.transpose, T.taut[:, 32 * k:32 * k + 32], p[5][:, k:256:8], ev=e_tt)
+    for k in range(2):
+        e_tauo[k] = V([e_tt], cp, T.tauo[:, 128 * k:128 * k + 128], T.taut[:, 128 * k:128 * k + 128])
 
     e_va = [act([e_tr, e_nl], T.vc[:, 64 * k:64 * k + 64], T.trs[:, :].indirect(T.nl[:, 4 * k:4 * k + 4]), F.Copy) for k in (0, 1)]
     e_vv = [V([e_tr, e_nl], cp, T.vc[:, 64 * k:64 * k + 64], T.trs[:, :].indirect(T.nl[:, 4 * k:4 * k + 4])) for k in (2, 3)]
@@ -160,48 +217,22 @@ def rank_program(g, core, T, topo):
     e_cs = run("P", [], lambda: mm)
     own = slice(32 * rank, 32 * rank + 32)
     e_own = V([e_cs], cp, T.cland[:, own], p[2][:, 0:32])
-    e_one16 = V([], vec.memset, T.one16[0:16, :], 1.0)
-
-    def along(q, c0, c1):
-        o, i = T.comp[:, 16 * c0:16 * c1], T.trs[:, :].indirect(T.tauo[:, c0:c1])
-        return V([e_tr, e_tauo], lambda: cp(o, i)) if q == "V" else act([e_tr, e_tauo], o, i, F.Copy)
-
-    e_c = [along("V", 0, 128), along("S", 128, 256)]
-
-    order = [(rank + 1 + t) % N for t in range(N)]
-    others = order[:-1]
-
-    def dst_id(q):
-        rid, pid, _ = topo.addr(T.cores[q])
-        return DstId(rid=rid, pnc=pid)
-
-    def bits(es):
-        m = 0
-        for e in es:
-            m |= 1 << e
-        return m
-
-    eng = [e for e in topo.engines(core, T.cores[others[0]]) if all(e in topo.engines(core, T.cores[q]) for q in others)]
     use("G", [e_own])
     g.remote_dma_fused([RemoteDMATransfer(dst_ids=[dst_id(q) for q in others], dma_engine_mask=bits(eng), remote_sem=T.sem["carr%d" % rank],
                                           srcs=[T.cland[:, own]], dsts=[T.cland[:, own] for q in others])], local_sem=T.sem.csent)
+    e_em = event()
+    for t, q, d, n in runs:
+        sel([e_ones], T.em[0:16, 32 * t:32 * t + 32 * n], T.ones[0:16, 0:32 * n], [[-2 * d, n], [-1, 2], [0, 16]], A.is_equal, -2 * q, 1, ev=e_em)
+    e_wc = iota_f(T.wc[0:1, :], [[16, 16]], 0)
 
-    e_n = {q: event() for q in "GVS"}
-
-    def reorder(q, pieces):
-        for r, h in pieces:
-            o, i = T.nat[:, 256 * r + 128 * h:256 * r + 128 * h + 128], T.comp[:, 2048 * h + r:2048 * h + 2048:16]
-            if q == "G":
-                sel([e_c[h]], o, i, [[0, 128]], A.is_equal, 0, 0, ev=e_n[q])
-            elif q == "V":
-                V([e_c[h]], cp, o, i, ev=e_n[q])
-            else:
-                act([e_c[h]], o, i, F.Copy, ev=e_n[q])
-
-    pieces = [(r, h) for h in range(2) for r in range(16)]
-    reorder("G", pieces[27:])
-    reorder("S", pieces[18:27])
-    reorder("V", pieces[:18])
+    e_n = {q: event() for q in "VS"}
+    for k in range(8):
+        q = "VS"[k // 4]
+        o, i = T.nat[:, k:4096:8], T.trs[:, :].indirect(T.tauo[:, 32 * k:32 * k + 32])
+        if q == "V":
+            V([e_tr, e_tauo[0]], cp, o, i, ev=e_n[q])
+        else:
+            act([e_tr, e_tauo[1]], o, i, F.Copy, ev=e_n[q])
 
     use("P", [e_own, e_ident])
     pe.matmul(p[3][:, 0:32], T.ident[:, :], T.cland[:, own], start=True, stop=False)
@@ -209,20 +240,20 @@ def rank_program(g, core, T, topo):
     use("P", [e_idf, e_dy2s, e_lxa])
     for k, (c0, c1) in enumerate(parts):
         pe.matmul(p[6 + k][:, 0:c1 - c0], T.identf[:, :], T.dy2s[:, c0:c1], start=True, stop=False)
-    for q in reversed(others):
+    for q in senders[:-1]:
         pe.wait_ge(T.sem["carr%d" % q], len(eng))
-        mm = pe.matmul(p[3][:, 0:32], T.ident[:, :], T.cland[:, 32 * q:32 * q + 32], start=False, stop=q == others[0])
+        mm = pe.matmul(p[3][:, 0:32], T.ident[:, :], T.cland[:, 32 * q:32 * q + 32], start=False, stop=q == senders[N - 2])
     e_tot = run("P", [], lambda: mm)
     e_sq = act([e_tot], T.sq[:, :], p[3][:, 0:32], F.Square)
     e_e = chain([e_sq, e_le], [lambda: pe.matmul(p[4][0:16, 0:16], T.le[:, 0:16], T.sq[:, 0:16], start=True, stop=False),
                                lambda: pe.matmul(p[4][0:16, 0:16], T.le[:, 16:32], T.sq[:, 16:32], start=False, stop=True)])
-    e_run = V([e_e, e_one16], vec.tensor_tensor_scan, T.run[0:16, :], T.one16[0:16, :], p[4][0:16, 0:16], 0.0, A.mult, A.max)
+    e_run = V([e_e, e_one64], vec.tensor_tensor_scan, T.run[0:16, :], T.one64[0:16, 0:16], p[4][0:16, 0:16], 0.0, A.mult, A.max)
     ac = T.acol[0:16, 0:1]
     e_ac = act([e_run], T.lt[0:16, :], T.run[0:16, :], F.Sign, bias=T.run[0:16, 15:16], scale=-1.0, accum_out=ac)
     e_d = []
     for k, (c0, c1) in enumerate(parts):
         e_a = V([e_ac, e_em], ts, T.dga[0:16, c0:c1], T.em[0:16, c0:c1], ac, None, A.mult)
-        e_b = V([], ts, T.dgb[0:16, c0:c1], T.em[0:16, c0:c1], ac, ac, A.mult, A.mult)
+        e_b = act([e_ac, e_em], T.dgb[0:16, c0:c1], T.em[0:16, c0:c1], F.Square, scale=ac)
         o = p[6 + k][:, 0:c1 - c0]
         use("P", [e_a])
         pe.matmul(o, T.lxa[0:16, :], T.dga[0:16, c0:c1], start=False, stop=False)
@@ -244,7 +275,7 @@ def rank_program(g, core, T, topo):
     def gather(q, t, j0=0, j1=512):
         o = T.ff[:, 512 * t + j0:512 * t + j1]
         i = T.nat[:, :].indirect(T.flist[:, 32 * t + j0 // 16:32 * t + j1 // 16])
-        w = [e_n["G"], e_n["V"], e_n["S"], e_sel[t]]
+        w = [e_n["V"], e_n["S"], e_sel[t]]
         e_f[t].append((j0, V(w, lambda: cp(o, i)) if q == "V" else act(w, o, i, F.Copy)))
 
     e_pt, last = {}, [None]
@@ -252,8 +283,7 @@ def rank_program(g, core, T, topo):
     def collect(k):
         pe.wait_ge(T.sem["far%d" % k], len(eng) // len(groups[k]) * len(groups[k]))
         for t in groups[k]:
-            q = (rank - 1 - t) % N
-            last[0] = pe.matmul(p[5][0:64, 0:128], T.fland[:, 64 * q:64 * q + 64], T.ident[:, :], start=t == 0, stop=t == N - 2)
+            last[0] = pe.matmul(p[5][0:64, 0:128], T.fland[:, 64 * senders[t]:64 * senders[t] + 64], T.ident[:, :], start=t == 0, stop=t == N - 2)
 
     def sensors(t):
         for c in range(4):
@@ -301,16 +331,10 @@ def rank_program(g, core, T, topo):
     gather("S", 6, 256, 512)
     send(3)
     sensors(6)
-    e_wfm = V([e_wfi], ts, T.wfm[:, :], T.wfi[:, :], 63, None, A.bitwise_and)
-    e_wf = V([e_wfm], ts, T.wf[:, :], T.wfm[:, :], 0.0, None, A.is_equal)
     send(4)
     gather("V", 7, 0, 128)
     gather("S", 7, 128, 512)
-    use("P", [e_sel[0]])
-    mm = pe.matmul(p[6][0:1, k0:16], T.ones[0:16, 0:1], T.dga[0:16, 0:16 * n1:16], start=True, stop=True)
-    if k0:
-        mm = pe.matmul(p[6][0:1, 0:k0], T.ones[0:16, 0:1], T.dga[0:16, 16 * n1:256:16], start=True, stop=True)
-    e_w1 = run("P", [], lambda: mm)
+    e_w1 = chain([e_ac, e_idf, e_sel[0]], [lambda: pe.matmul(p[6][0:1, 0:16], ac, T.identf[0:16, 0:16], start=True, stop=True)])
     collect(0)
     collect(1)
     sensors(7)
@@ -323,6 +347,7 @@ def rank_program(g, core, T, topo):
     e_y = V([e_fin], cp, T.ysb[0:64, :], p[5][0:64, 0:128])
     e_st = run("Y", [e_y], lambda: g.sync.dma_start(T.y[:, :], T.ysb[0:64, :]), inc=16)
     use("Y", [e_w, e_st])
+    g.wait_ge(T.sem.ssent, len(eng))
     g.wait_ge(T.sem.csent, len(eng))
     g.wait_ge(T.sem.fsent, len(groups) * len(eng))
     for e in events:

from concourse.bass import DstId, RemoteDMATransfer
from concourse.mybir import AluOpType as A, ActivationFunctionType as F

_SB = {
    "int32": "posi 2 taus 256 vi 128 e8s 128 pgi 2 wdi 16 wdm 16 pcol 2 rcol 2 r4 2 d2w 16 lo32 16 d2i 256 hi 256",
    "uint16": "tauo 256 lo 16 nl 16 flist 256",
    "bfloat16": "posf 2 trs 8192 nat 4096 e8 128 ones 256 ident 128 wd 144 wf 80 vc 256 cland 256 xq 16 lxa 128 lxb 128 em 256 "
                "dga 256 dgb 256 ff 4096 fsend 448 fland 512",
    "float32": "negp 2 lw 140 pgf 2 pf 2 rf 2 c16 2 c4 2 dyw 2 yy 256 xx 256 yrot 256 sy 256 t1 16 sw 16 "
               "hm 256 prod 256 dg 64 dd 64 a3 32 a4 16 dy2 256 dy2s 256 dx2 2 dxs 2 rfree 128 le 32 identf 128 sq 32 "
               "one64 64 pw 260 tauf 256 taut 256 run 16 lt 16 acol 2 wc 16 w2 16 ysb 128",
}
SCRATCH = {"p%d" % _k: ("psum", [128, 512], "float32") for _k in range(8)}
for _d in _SB:
    _l = _SB[_d].split()
    for _k in range(0, len(_l), 2):
        SCRATCH[_l[_k]] = ("sbuf", [128, int(_l[_k + 1])], _d)
SEMAPHORES = ["carr%d" % _k for _k in range(8)] + ["far%d" % _k for _k in range(5)] + ["csent", "fsent", "shared", "ssent"] + ["e%d" % _k for _k in range(130)]


def rank_program(g, core, T, topo):
    rank = T.rank_of(core)
    if rank is None:
        return
    N = len(T.cores)
    vec, sca, pe = g.vector, g.scalar, g.tensor
    queues = {"G": g, "V": vec, "S": sca, "P": pe, "Y": g.sync}
    known = {q: set() for q in queues}
    events = []

    def event():
        e = {"n": len(events), "sem": T.sem["e%d" % len(events)], "total": 0, "knows": set(), "used": False}
        events.append(e)
        return e

    def use(q, waits):
        for e in waits:
            if e["n"] not in known[q]:
                queues[q].wait_ge(e["sem"], e["total"])
                e["used"] = True
                known[q] |= e["knows"] | {e["n"]}

    def run(q, waits, call, ev=None, inc=1):
        use(q, waits)
        e = event() if ev is None else ev
        assert not e["used"]
        call().then_inc(e["sem"], inc)
        e["total"] += inc
        e["knows"] |= known[q]
        return e

    def V(waits, fn, *a, **k):
        return run("V", waits, lambda: fn(*a), **k)

    ts, tt, cp = vec.tensor_scalar, vec.tensor_tensor, vec.tensor_copy
    act = lambda waits, out, in_, func, ev=None, **k: run("S", waits, lambda: sca.activation(out, in_, func, **k), ev=ev)

    def chain(waits, mms):
        use("P", waits)
        for m in mms:
            last = m()
        return run("P", [], lambda: last)

    p = [T["p%d" % k] for k in range(8)]

    e_pos = run("Y", [], lambda: g.sync.dma_start(T.posi[0:8, :], T.pos[:, :]), inc=16)
    e_tau = run("S", [], lambda: sca.dma_start(T.taus[:, :], T.tau[:, :]), inc=16)
    e_tr = run("Y", [], lambda: g.sync.dma_start(T.trs[:, :], T.tr[:, :]), inc=16)

    def kind(a, b):
        a, b = topo.chip(T.cores[a]), topo.chip(T.cores[b])
        return 2 if topo.mates(a, b) else 1 if topo.same_plane(a, b) else 0

    def ordered(r):
        return sorted([q for q in range(N) if q != r], key=lambda q: (kind(r, q), (q - r) % N)) + [r]

    order = ordered(rank)
    others, mate = order[:-1], order[-2]
    senders = [[q for q in range(N) if ordered(q)[t] == rank][0] for t in range(N)]

    def dst_id(q):
        rid, pid, _ = topo.addr(T.cores[q])
        return DstId(rid=rid, pnc=pid)

    def bits(es):
        m = 0
        for e in es:
            m |= 1 << e
        return m

    eng = [e for e in topo.engines(core, T.cores[mate]) if all(e in topo.engines(core, T.cores[q]) for q in others)]

    runs, t = [], 0
    while t < N:
        n, d = 1, (order[t + 1] - order[t] if t + 1 < N else 1)
        while t + n < N and order[t + n] == order[t] + n * d:
            n += 1
        runs.append((t, order[t], d, n))
        t += n

    iota_i = lambda out, pat, base, cm: run("G", [], lambda: g.iota(out, pat, base, cm))
    iota_f = lambda out, pat, base, ev=None: run("G", [], lambda: g.iota(out, pat, base, 0, allow_small_or_imprecise_dtypes=True), ev=ev)
    sel = lambda waits, out, in_, pat, op, base, cm, ev=None: run("G", waits, lambda: g.affine_select(out, in_, pat, op, 0.0, base, cm), ev=ev)
    e_one64 = V([], vec.memset, T.one64[:, :], 1.0)
    e_ones = V([], vec.memset, T.ones[:, :], 1.0)
    e_wd0 = V([], vec.memset, T.wd[:, :], 0.0)
    e_pw0 = V([], vec.memset, T.pw[:, :], 0.0)
    e_tab0 = V([], vec.memset, T.wf[:, :] if rank < mate else T.le[:, :], 0.0)
    e_pcol = iota_i(T.pcol[:, 0:1], [[1, 1]], 0, 1)
    e_vi = iota_i(T.vi[:, :], [[1, 8], [16, 4], [0, 4]], 0, 0)
    e_yy = iota_f(T.yy[:, :], [[0, 16], [16, 16]], 8)
    e_xx = iota_f(T.xx[:, :], [[16, 16], [0, 16]], 8)
    e_pw = event()
    for o in range(2):
        sel([e_one64, e_pw0], T.pw[:, 130 * o + 1:130 * o + 129:2], T.one64[:, :], [[-32, 4], [-1, 16]], A.is_equal, -16 * o, 1, ev=e_pw)
    e_wdi = iota_i(T.wdi[:, :], [[1, 16]], 128, -1)
    e_ident = sel([e_ones], T.ident[:, :], T.ones[:, 0:128], [[-1, 128]], A.is_equal, 0, 1)

    e_r = V([e_pcol], ts, T.rcol[:, 0:1], T.pcol[:, 0:1], 15, None, A.bitwise_and)
    e_pgi = V([], ts, T.pgi[:, 0:1], T.pcol[:, 0:1], 4, None, A.arith_shift_right)
    e_pf = V([], cp, T.pf[:, 0:1], T.pcol[:, 0:1])
    e_e8s = V([e_vi], ts, T.e8s[0:8, :], T.vi[0:8, :], 15, None, A.bitwise_and)
    e_pgf = V([e_pgi], cp, T.pgf[:, 0:1], T.pgi[:, 0:1])
    e_e8 = V([e_e8s, e_pf], ts, T.e8[0:8, :], T.e8s[0:8, :], T.pf[0:8, 0:1], -1.0, A.is_equal, A.mult)
    e_c16 = V([e_r], ts, T.c16[:, 0:1], T.rcol[:, 0:1], 16.0, 8.0, A.mult, A.add)

    e_posf = V([e_pos], cp, T.posf[0:8, :], T.posi[0:8, :])
    e_pb = run("P", [e_e8, e_posf], lambda: pe.matmul(p[0][:, 0:2], T.e8[0:8, :], T.posf[0:8, :], start=True, stop=True))
    e_rf = V([e_r], cp, T.rf[:, 0:1], T.rcol[:, 0:1])
    e_xq = V([e_posf, e_ones], ts, T.xq[0:8, :], T.ones[0:8, 0:16], T.posf[0:8, 0:1], None, A.mult)
    e_np = V([e_pb], cp, T.negp[:, :], p[0][:, 0:2])
    nx, ny = T.negp[:, 0:1], T.negp[:, 1:2]
    e_dyw = act([e_c16, e_np], T.dyw[:, 0:1], T.c16[:, 0:1], F.Square, bias=ny)
    e_sy = act([e_yy], T.sy[:, :], T.yy[:, :], F.Square, bias=ny)
    e_sx = act([e_xx], p[6][:, 0:256], T.xx[:, :], F.Square, bias=nx)
    e_pq = run("P", [e_xq], lambda: pe.matmul(p[7][0:16, 0:128], T.xq[0:8, :], T.e8[0:8, :], start=True, stop=True))

    e_t1 = V([e_yy, e_np], ts, T.t1[:, :], T.yy[:, 0:16], nx, None, A.add)
    e_l = event()
    V([], vec.memset, T.lw[:, 0:12], 0.0, ev=e_l)
    e_sw = V([e_t1], tt, T.sw[:, :], T.t1[:, :], T.t1[:, :], A.mult)
    V([e_vi, e_pgf], ts, T.lw[:, 12:140], T.vi[:, :], T.pgf[:, 0:1], None, A.is_equal, ev=e_l)
    e_d2w = V([e_sw, e_dyw], ts, T.d2w[:, :], T.sw[:, :], T.dyw[:, 0:1], None, A.add)

    e_tauf = V([e_tau], cp, T.tauf[:, :], T.taus[:, :])

    def pairs(o):
        use("P", [e_tauf, e_pw])
        for x in range(2):
            mm = pe.matmul(p[5][:, 128 * o:128 * o + 128], T.pw[:, 130 * o + 1 - x:130 * o + 129 - x], T.tauf[:, 128 * x:128 * x + 128],
                           start=x == 0, stop=x == 1)
        return run("P", [], lambda: mm)

    pairs(0)
    e_lo32 = V([e_d2w], ts, T.lo32[:, :], T.d2w[:, :], 5, 255, A.arith_shift_right, A.bitwise_and)
    e_lo = V([e_lo32], cp, T.lo[:, :], T.lo32[:, :])
    e_wdm = V([e_wdi], ts, T.wdm[:, :], T.wdi[:, :], 15, None, A.bitwise_and)
    e_d2i = V([e_sx, e_sy], tt, T.d2i[:, :], p[6][:, 0:256], T.sy[:, :], A.add)
    e_hi = V([e_d2i], ts, T.hi[:, :], T.d2i[:, :], 13, None, A.arith_shift_right)

    e_shared = {"n": len(events), "sem": T.sem.shared, "total": len(eng), "knows": set(), "used": False}
    events.append(e_shared)
    if rank < mate:
        e_made = V([e_wdm, e_tab0], ts, T.wf[:, 3:67:4], T.wdm[:, :], 0.0, None, A.is_equal)
        e_wf, e_le, table = e_made, e_shared, T.wf
    else:
        e_made = event()
        for h in range(2):
            sel([e_l, e_tab0], T.le[:, 17 * h:17 * h + 15:2], T.lw[:, 12:140:16], [[0, 8]], A.is_equal, 0, 0, ev=e_made)
        e_wf, e_le, table = e_shared, e_made, T.le
    use("G", [e_made])
    g.remote_dma_fused([RemoteDMATransfer(dst_ids=[dst_id(mate)], dma_engine_mask=bits(eng), remote_sem=T.sem.shared,
                                          srcs=[table[:, :]], dsts=[table[:, :]])], local_sem=T.sem.ssent)
    e_yrot = event()
    for t, q, d, n in runs:
        iota_f(T.yrot[:, 32 * t:32 * t + 32 * n], [[32 * d, n], [1, 32]], 32 * q, ev=e_yrot)
    e_rfree = iota_f(T.rfree[0:16, :], [[0, 8], [1, 16]], 0)

    e_hm = V([e_hi, e_rf], ts, T.hm[:, :], T.hi[:, :], T.rf[:, 0:1], None, A.is_equal)
    e_prod = [V([e_hm, e_lo, e_tau], lambda k=k: tt(T.prod[:, 128 * k:128 * k + 128], T.taus[:, :].indirect(T.lo[:, 8 * k:8 * k + 8]),
                                                    T.hm[:, 128 * k:128 * k + 128], A.mult)) for k in range(2)]
    for q in range(4):
        use("P", [e_prod[q // 2], e_l])
        mm = pe.matmul(p[1][:, 0:64], T.lw[:, 12 - 4 * q:140 - 4 * q], T.prod[:, 64 * q:64 * q + 64], start=q == 0, stop=q == 3)
    e_s = run("P", [], lambda: mm)
    e_z = pairs(1)

    e_dx2 = act([e_rf], T.dx2[:, 0:1], T.rf[:, 0:1], F.Square, bias=nx)
    e_dxs = act([e_dx2], T.dxs[:, 0:1], T.dx2[:, 0:1], F.Copy, bias=-15.5 / 32, scale=1.0 / 32)
    e_idf = act([e_ident], T.identf[:, :], T.ident[:, :], F.Copy)
    e_dy2 = act([e_yrot], T.dy2[:, :], T.yrot[:, :], F.Square, bias=ny)
    e_dy2s = act([e_dxs, e_dy2], T.dy2s[:, :], T.dy2[:, :], F.Identity, bias=T.dxs[:, 0:1], scale=1.0 / 32)
    e_r4 = V([], ts, T.r4[:, 0:1], T.pcol[:, 0:1], 3, None, A.bitwise_and)
    e_wd = V([e_wdm, e_wd0], ts, T.wd[:, 16:32], T.wdm[:, :], 0.0, None, A.is_equal)
    e_c4 = V([e_r4], ts, T.c4[:, 0:1], T.r4[:, 0:1], 16.0, 8.0, A.mult, A.add)
    e_dg = V([e_xx, e_c4], ts, T.dg[:, :], T.xx[:, 0:64], T.c4[:, 0:1], None, A.is_equal)
    e_dd = V([e_s, e_dg], tt, T.dd[:, :], p[1][:, 0:64], T.dg[:, :], A.mult)
    e_a3 = V([e_dd], tt, T.a3[:, :], T.dd[:, 0:32], T.dd[:, 32:64], A.add)
    e_a4 = V([e_a3], tt, T.a4[:, :], T.a3[:, 0:16], T.a3[:, 16:32], A.add)
    e_nl = V([e_a4], cp, T.nl[:, :], T.a4[:, :])

    e_tt, e_tauo = event(), [None, None]
    for k in range(8):
        V([e_z], vec.transpose, T.taut[:, 32 * k:32 * k + 32], p[5][:, k:256:8], ev=e_tt)
    for k in range(2):
        e_tauo[k] = V([e_tt], cp, T.tauo[:, 128 * k:128 * k + 128], T.taut[:, 128 * k:128 * k + 128])

    e_va = [act([e_tr, e_nl], T.vc[:, 64 * k:64 * k + 64], T.trs[:, :].indirect(T.nl[:, 4 * k:4 * k + 4]), F.Copy) for k in (0, 1)]
    e_vv = [V([e_tr, e_nl], cp, T.vc[:, 64 * k:64 * k + 64], T.trs[:, :].indirect(T.nl[:, 4 * k:4 * k + 4])) for k in (2, 3)]
    e_lxa = V([e_pq, e_rfree], tt, T.lxa[0:16, :], p[7][0:16, 0:128], T.rfree[0:16, :], A.add)
    e_lxb = V([], vec.memset, T.lxb[0:16, :], 8.0)
    use("P", [e_wd])
    for k in (0, 1, 4, 5, 2, 3, 6, 7):
        use("P", [(e_va + e_vv)[k // 2]])
        o = 32 * (k // 2)
        mm = pe.matmul(p[2][o:o + 32, 0:32], T.wd[:, 16 - 16 * (k % 2):48 - 16 * (k % 2)], T.vc[:, 32 * k:32 * k + 32], start=k % 2 == 0, stop=k % 2 == 1)
    e_cs = run("P", [], lambda: mm)
    own = slice(32 * rank, 32 * rank + 32)
    e_own = V([e_cs], cp, T.cland[:, own], p[2][:, 0:32])
    use("G", [e_own])
    g.remote_dma_fused([RemoteDMATransfer(dst_ids=[dst_id(q) for q in others], dma_engine_mask=bits(eng), remote_sem=T.sem["carr%d" % rank],
                                          srcs=[T.cland[:, own]], dsts=[T.cland[:, own] for q in others])], local_sem=T.sem.csent)
    e_em = event()
    for t, q, d, n in runs:
        sel([e_ones], T.em[0:16, 32 * t:32 * t + 32 * n], T.ones[0:16, 0:32 * n], [[-2 * d, n], [-1, 2], [0, 16]], A.is_equal, -2 * q, 1, ev=e_em)
    e_wc = iota_f(T.wc[0:1, :], [[16, 16]], 0)

    e_n = {q: event() for q in "VS"}
    for k in range(8):
        q = "VS"[k // 4]
        o, i = T.nat[:, k:4096:8], T.trs[:, :].indirect(T.tauo[:, 32 * k:32 * k + 32])
        if q == "V":
            V([e_tr, e_tauo[0]], cp, o, i, ev=e_n[q])
        else:
            act([e_tr, e_tauo[1]], o, i, F.Copy, ev=e_n[q])

    use("P", [e_own, e_ident])
    pe.matmul(p[3][:, 0:32], T.ident[:, :], T.cland[:, own], start=True, stop=False)
    parts = [(0, 64), (64, 256)]
    use("P", [e_idf, e_dy2s, e_lxa])
    for k, (c0, c1) in enumerate(parts):
        pe.matmul(p[6 + k][:, 0:c1 - c0], T.identf[:, :], T.dy2s[:, c0:c1], start=True, stop=False)
    for q in senders[:-1]:
        pe.wait_ge(T.sem["carr%d" % q], len(eng))
        mm = pe.matmul(p[3][:, 0:32], T.ident[:, :], T.cland[:, 32 * q:32 * q + 32], start=False, stop=q == senders[N - 2])
    e_tot = run("P", [], lambda: mm)
    e_sq = act([e_tot], T.sq[:, :], p[3][:, 0:32], F.Square)
    e_e = chain([e_sq, e_le], [lambda: pe.matmul(p[4][0:16, 0:16], T.le[:, 0:16], T.sq[:, 0:16], start=True, stop=False),
                               lambda: pe.matmul(p[4][0:16, 0:16], T.le[:, 16:32], T.sq[:, 16:32], start=False, stop=True)])
    e_run = V([e_e, e_one64], vec.tensor_tensor_scan, T.run[0:16, :], T.one64[0:16, 0:16], p[4][0:16, 0:16], 0.0, A.mult, A.max)
    ac = T.acol[0:16, 0:1]
    e_ac = act([e_run], T.lt[0:16, :], T.run[0:16, :], F.Sign, bias=T.run[0:16, 15:16], scale=-1.0, accum_out=ac)
    e_d = []
    for k, (c0, c1) in enumerate(parts):
        e_a = V([e_ac, e_em], ts, T.dga[0:16, c0:c1], T.em[0:16, c0:c1], ac, None, A.mult)
        e_b = act([e_ac, e_em], T.dgb[0:16, c0:c1], T.em[0:16, c0:c1], F.Square, scale=ac)
        o = p[6 + k][:, 0:c1 - c0]
        use("P", [e_a])
        pe.matmul(o, T.lxa[0:16, :], T.dga[0:16, c0:c1], start=False, stop=False)
        e_d.append(chain([e_b, e_lxb], [lambda: pe.matmul(o, T.lxb[0:16, :], T.dgb[0:16, c0:c1], start=False, stop=True)]))

    e_sel = {}

    def select(k):
        t0, t1 = parts[k][0] // 32, parts[k][1] // 32
        e = V([e_d[k]], cp, T.flist[:, 32 * t0:32 * t1], p[6 + k][:, 0:32 * (t1 - t0)])
        for t in range(t0, t1):
            e_sel[t] = e

    groups = [[0], [1], [2, 3], [4, 5], [6]]
    banks = [p[0], p[1], p[2], p[3], p[4]]
    at = {t: (k, tts.index(t)) for k, tts in enumerate(groups) for t in tts}
    e_f = {t: [] for t in range(N)}

    def gather(q, t, j0=0, j1=512):
        o = T.ff[:, 512 * t + j0:512 * t + j1]
        i = T.nat[:, :].indirect(T.flist[:, 32 * t + j0 // 16:32 * t + j1 // 16])
        w = [e_n["V"], e_n["S"], e_sel[t]]
        e_f[t].append((j0, V(w, lambda: cp(o, i)) if q == "V" else act(w, o, i, F.Copy)))

    e_pt, last = {}, [None]

    def collect(k):
        pe.wait_ge(T.sem["far%d" % k], len(eng) // len(groups[k]) * len(groups[k]))
        for t in groups[k]:
            last[0] = pe.matmul(p[5][0:64, 0:128], T.fland[:, 64 * senders[t]:64 * senders[t] + 64], T.ident[:, :], start=t == 0, stop=t == N - 2)

    def sensors(t):
        for c in range(4):
            use("P", [e for j0, e in e_f[t] if j0 < 128 * c + 128] + [e_wd])
            f = T.ff[:, 512 * t + 128 * c:512 * t + 128 * c + 128]
            if t == N - 1:
                use("P", [e_wf])
                pe.matmul(p[5][0:64, 0:128], T.wf[:, 3 - c:67 - c], f, start=False, stop=False)
            else:
                o = 64 * at[t][1]
                mm = pe.matmul(banks[at[t][0]][:, o + c:o + 64:4], f, T.wd[:, 16:32], start=True, stop=True)
        if t < N - 1:
            e_pt[t] = run("P", [], lambda: mm)

    def send(k):
        tts = groups[k]
        e = V([e_pt[t] for t in tts], cp, T.fsend[:, 64 * tts[0]:64 * tts[-1] + 64], banks[k][:, 0:64 * len(tts)])
        use("G", [e])
        n = len(eng) // len(tts)
        g.remote_dma_fused([RemoteDMATransfer(dst_ids=[dst_id(order[t])], dma_engine_mask=bits(eng[n * i:n * i + n]), remote_sem=T.sem["far%d" % k],
                                              srcs=[T.fsend[:, 64 * t:64 * t + 64]], dsts=[T.fland[:, 64 * rank:64 * rank + 64]])
                            for i, t in enumerate(tts)], local_sem=T.sem.fsent)

    select(0)
    gather("V", 0, 0, 256)
    gather("S", 0, 256, 512)
    sensors(0)
    select(1)
    gather("V", 1, 0, 256)
    gather("S", 1, 256, 512)
    send(0)
    sensors(1)
    gather("S", 2)
    sensors(2)
    gather("V", 3)
    send(1)
    sensors(3)
    gather("S", 4)
    sensors(4)
    gather("V", 5, 0, 320)
    send(2)
    gather("S", 5, 320, 512)
    sensors(5)
    gather("V", 6, 0, 256)
    gather("S", 6, 256, 512)
    send(3)
    sensors(6)
    send(4)
    gather("V", 7, 0, 128)
    gather("S", 7, 128, 512)
    e_w1 = chain([e_ac, e_idf, e_sel[0]], [lambda: pe.matmul(p[6][0:1, 0:16], ac, T.identf[0:16, 0:16], start=True, stop=True)])
    collect(0)
    collect(1)
    sensors(7)
    e_w2 = V([e_w1, e_wc], tt, T.w2[0:1, :], p[6][0:1, 0:16], T.wc[0:1, :], A.add)
    e_w = run("Y", [e_w2], lambda: g.sync.dma_start(T.w[:, :], T.w2[0:1, :]), inc=16)

    for k in range(2, len(groups)):
        collect(k)
    e_fin = run("P", [], lambda: last[0])
    e_y = V([e_fin], cp, T.ysb[0:64, :], p[5][0:64, 0:128])
    e_st = run("Y", [e_y], lambda: g.sync.dma_start(T.y[:, :], T.ysb[0:64, :]), inc=16)
    use("Y", [e_w, e_st])
    g.wait_ge(T.sem.ssent, len(eng))
    g.wait_ge(T.sem.csent, len(eng))
    g.wait_ge(T.sem.fsent, len(groups) * len(eng))
    for e in events:
        if not e["used"]:
            g.wait_ge(e["sem"], e["total"])
